import numpy as np
import ml_dtypes


def mxq(x, axis, fmt="e4m3"):
    dtype, down = {"e4m3": (ml_dtypes.float8_e4m3fn, 7), "e5m2": (ml_dtypes.float8_e5m2, 14)}[fmt]
    v = np.moveaxis(np.asarray(x, np.float32).astype(ml_dtypes.bfloat16).astype(np.float64), axis, -1)
    blocks = v.reshape(v.shape[:-1] + (-1, 32))
    amax = np.abs(blocks).max(-1, keepdims=True)
    byte = np.maximum(np.where(amax > 0, np.frexp(amax)[1] - 1 + 127, 0) - down, 1)
    scale = np.exp2(byte - 127.0)
    codes = (blocks / scale).astype(np.float32).astype(dtype).astype(np.float64)
    return np.moveaxis((codes * scale).reshape(v.shape), -1, axis)


WIDE = False


def mx_kscale(k):
    if not WIDE:
        return np.ones(k)
    levels = np.array([10, -10, 5, -5, 0])
    if k % 512:
        return np.exp2(np.random.permutation(np.resize(levels, k // 32))).repeat(32)
    a = np.empty((k // 512, 16))
    for p in range(k // 512):
        a[p, :8] = np.random.permutation(np.resize(levels, 8))
        for g in range(8):
            far = levels[np.abs(levels - a[p, g]) >= 10]
            a[p, g + 8] = far[np.random.randint(len(far))]
    return np.exp2(a.ravel()).repeat(32)


def f64(x):
    return np.asarray(x).astype(np.float64)


def striped(idx):
    return np.tile(idx.reshape(-1, 16).T, (8, 1)).astype(np.uint16)


def unstriped(offs):
    return offs[:16].T.reshape(-1).astype(np.int64)


def relu2(v):
    return np.maximum(v, 0.0) ** 2


K, T, D, S, V, N = 512, 2048, 3, 1024, 512, 128


def setup_inputs():
    n = np.random.standard_normal
    s = mx_kscale(K)[:, None]
    return {
        "xT": (n((K, T)) * s).astype(np.float32),
        "w": (n((K, N)) / np.sqrt(K) / s).astype(np.float32),
        "b": (0.3 * n((N, 1))).astype(np.float32),
        "gate": np.tile(np.random.uniform(0.2, 1.0, (D, 1, V)) / np.sqrt(D), (1, N, 1)).astype(np.float32),
        "offs": striped(np.random.permutation(T)[:S]),
        "pos1": striped(np.random.permutation(S)[:V]),
        "pos2": striped(np.random.permutation(S)[:V]),
        "pos3": striped(np.random.permutation(S)[:V]),
    }


def reference(xT, w, b, gate, offs, pos1, pos2, pos3):
    idx = unstriped(offs)
    xq = mxq(f64(xT)[:, idx], 0, "e4m3")
    y = mxq(f64(w), 0, "e4m3").T @ xq
    y = relu2(y + f64(b))
    return sum(f64(gate[d]) * y[:, unstriped(p)] for d, p in enumerate((pos1, pos2, pos3)))

@@ -1,0 +1,167 @@
+from contextlib import ExitStack
+
+import concourse.mybir as mybir
+from concourse.masks import make_identity
+
+K, T, D, S, V, N = 512, 2048, 3, 1024, 512, 128
+P = 128
+FLOPS = 2 * K * N * S
+
+F32 = mybir.dt.float32
+BF16 = mybir.dt.bfloat16
+U32 = mybir.dt.uint32
+U16 = mybir.dt.uint16
+U8 = mybir.dt.uint8
+FP8X4 = mybir.dt.float8_e4m3fn_x4
+ACT = mybir.ActivationFunctionType
+ALU = mybir.AluOpType
+
+LOADS = (((0, 1024), (1024, 1024)), ((0, 1024), (1024, 768), (1792, 256)))
+PIECES = ((0, 256), (256, 256), (512, 256), (768, 256))
+WARM = 24
+PLAIN = {0: "S", 1: "G"}
+
+
+def tile_picked_sub_lin_relu2_sub_e_kernel(tc, xT, w, b, gate, offs, pos1, pos2, pos3, out):
+    nc = tc.nc
+    with ExitStack() as ctx:
+        keep = ctx.enter_context(tc.tile_pool(name="keep", bufs=1))
+        psum = ctx.enter_context(tc.psum_pool(name="psum", bufs=1))
+
+        raw = [[keep.tile([P, 2, n], F32, name=f"raw_{u}_{a}") for (a, n) in LOADS[u]] for u in range(2)]
+        pairs = [keep.tile([P, T, 2], BF16, name=f"pairs_{u}", align_bytes=64) for u in range(2)]
+        offsets = keep.tile([P, S // 16], U16, name="offsets")
+        lists = [keep.tile([P, V // 16], U16, name=f"list_{d}") for d in range(D)]
+        gates = [keep.tile([P, V], F32, name=f"gate_{d}") for d in range(D)]
+        w_raw = keep.tile([P, 4, N], F32, name="w_raw")
+        w_grouped = keep.tile([P, N, 4], BF16, name="w_grouped", align_bytes=64)
+        w_codes = keep.tile([P, N], U32, name="w_codes", align_bytes=64)
+        w_scales = keep.tile([P, N], U8, name="w_scales", align_bytes=64)
+        bias = keep.tile([P, 1], F32, name="bias")
+        grouped = [keep.tile([P, n, 4], BF16, name=f"grouped_{i}", align_bytes=64) for i, (a, n) in enumerate(PIECES)]
+        planar = {i: keep.tile([P, 2, PIECES[i][1]], U32, name=f"planar_{i}") for i in PLAIN}
+        codes = [keep.tile([P, n], U32, name=f"codes_{i}", align_bytes=64) for i, (a, n) in enumerate(PIECES)]
+        scales = [keep.tile([P, n], U8, name=f"scales_{i}", align_bytes=64) for i, (a, n) in enumerate(PIECES)]
+        rect = [keep.tile([P, n], F32, name=f"rect_{i}") for i, (a, n) in enumerate(PIECES)]
+        y = keep.tile([P, S], F32, name="y")
+        turns = [keep.tile([P, V], F32, name=f"turn_{d}") for d in range(D)]
+        partial = keep.tile([P, V], F32, name="partial")
+        result = keep.tile([P, V], F32, name="result")
+        acc = [psum.tile([P, n], F32, name=f"acc_{i}") for i, (a, n) in enumerate(PIECES)]
+
+        identity = keep.tile([P, P], BF16, name="identity", align_bytes=64)
+        make_identity(nc, identity[:])
+        warm = [psum.tile([P, 8, P], BF16, name=f"warm_{i}") for i in range(2)]
+
+        x_view = xT.rearrange("(p u j) t -> u p j t", u=2, j=2)
+        for u in range(2):
+            for c, (a, n) in enumerate(LOADS[u]):
+                nc.sync.dma_start(raw[u][c][:], x_view[u, :, :, a : a + n])
+            if u == 0:
+                nc.sync.dma_start(offsets[:], offs)
+        nc.sync.dma_start(w_raw[:], w.rearrange("(p j) n -> p j n", j=4))
+        nc.sync.dma_start(bias[:], b)
+        for d, pos in enumerate((pos1, pos2, pos3)):
+            nc.sync.dma_start(lists[d][:], pos)
+        for d in range(D):
+            nc.sync.dma_start(gates[d][:], gate[d])
+
+        def cast(engine, u, c, lo, hi):
+            a, n = LOADS[u][c]
+            dst = pairs[u][:, a + lo : a + hi, :]
+            src = raw[u][c][:, :, lo:hi].rearrange("p j t -> p t j")
+            if engine == "S":
+                nc.scalar.activation(dst, src, ACT.Copy)
+            else:
+                nc.vector.tensor_copy(dst, src)
+
+        def gather(u, i):
+            a, n = PIECES[i]
+            words = grouped[i][:].rearrange("p n k -> p (n k)").bitcast(U32).rearrange("p (n u) -> p n u", u=2)
+            window = pairs[u][:].rearrange("p t e -> p (t e)").bitcast(U32)
+            dst = planar[i][:, u, :] if i in PLAIN else words[:, :, u]
+            nc.vector.tensor_copy(dst, window.indirect(offsets[:, a // 16 : (a + n) // 16]))
+
+        def interleave(i):
+            src = planar[i][:].rearrange("p u n -> p (u n)").bitcast(BF16)
+            dst = grouped[i][:].rearrange("p n (u e) -> p n u e", u=2)
+            src = src.rearrange("p (u n e) -> p n u e", u=2, e=2)
+            if PLAIN[i] == "S":
+                nc.scalar.copy(dst, src)
+            else:
+                nc.gpsimd.tensor_scalar(dst, src, 1.0, 0.0, ALU.mult, ALU.add)
+
+        def quantize(i):
+            nc.vector.quantize_mx(
+                out=codes[i][:].bitcast(FP8X4), scales=scales[i][:], in_=grouped[i][:].rearrange("p n k -> p (n k)")
+            )
+
+        def multiply(i):
+            nc.tensor.matmul_mx(
+                out=acc[i][:],
+                lhsT=w_codes[:].bitcast(FP8X4),
+                lhsT_scale=w_scales[:],
+                rhs=codes[i][:].bitcast(FP8X4),
+                rhs_scale=scales[i][:],
+                start=True,
+                stop=True,
+            )
+
+        def relu(engine, i, lo, hi):
+            if engine == "S":
+                nc.scalar.activation(rect[i][:, lo:hi], acc[i][:, lo:hi], ACT.Relu, bias=bias[:, 0:1])
+            else:
+                nc.vector.tensor_scalar(rect[i][:, lo:hi], acc[i][:, lo:hi], bias[:, 0:1], 0.0, ALU.add, ALU.max)
+
+        def square(engine, i, lo, hi):
+            a, n = PIECES[i]
+            if engine == "S":
+                nc.scalar.activation(y[:, a + lo : a + hi], rect[i][:, lo:hi], ACT.Square)
+            else:
+                nc.vector.tensor_tensor(y[:, a + lo : a + hi], rect[i][:, lo:hi], rect[i][:, lo:hi], ALU.mult)
+
+        cast("S", 0, 0, 0, 640)
+        cast("V", 0, 0, 640, 1024)
+        cast("S", 0, 1, 0, 352)
+        cast("V", 0, 1, 352, 1024)
+        for i in range(4):
+            gather(0, i)
+        cast("S", 1, 0, 0, 512)
+        cast("S", 1, 0, 512, 1024)
+        cast("V", 1, 1, 0, 640)
+        cast("S", 1, 1, 640, 768)
+        cast("V", 1, 2, 0, 176)
+        cast("S", 1, 2, 176, 256)
+        nc.gpsimd.tensor_scalar(w_grouped[:], w_raw[:].rearrange("p j n -> p n j"), 1.0, 0.0, ALU.mult, ALU.add)
+        last = pairs[1][:].rearrange("p t e -> p (t e)")
+        for i in range(WARM):
+            at = 2 * 1792 + (i % 4) * P
+            nc.tensor.transpose(warm[(i // 8) % 2][:, i % 8, :], last[:, at : at + P], identity[:])
+        for i in range(4):
+            gather(1, i)
+        interleave(0)
+        interleave(1)
+        nc.vector.quantize_mx(
+            out=w_codes[:].bitcast(FP8X4), scales=w_scales[:], in_=w_grouped[:].rearrange("p n j -> p (n j)")
+        )
+        for i in (2, 3, 0, 1):
+            quantize(i)
+            multiply(i)
+        relu("S", 2, 0, 256)
+        square("S", 2, 0, 256)
+        relu("S", 3, 0, 256)
+        square("S", 3, 0, 256)
+        relu("V", 0, 0, 256)
+        relu("V", 1, 0, 256)
+        square("S", 0, 0, 256)
+        square("V", 1, 0, 128)
+        square("S", 1, 128, 256)
+
+        for d in range(D):
+            nc.vector.tensor_tensor(turns[d][:], y[:].indirect(lists[d][:]), gates[d][:], ALU.mult)
+        halves = (slice(0, 256), slice(256, 512))
+        for h in halves:
+            nc.vector.tensor_tensor(partial[:, h], turns[0][:, h], turns[1][:, h], ALU.add)
+        for h in halves:
+            nc.vector.tensor_tensor(result[:, h], partial[:, h], turns[2][:, h], ALU.add)
+            nc.sync.dma_start(out[:, h], result[:, h])

@@ -1,7 +1,6 @@
 from contextlib import ExitStack
 
 import concourse.mybir as mybir
-from concourse.masks import make_identity
 
 K, T, D, S, V, N = 512, 2048, 3, 1024, 512, 128
 P = 128
@@ -16,10 +15,11 @@ FP8X4 = mybir.dt.float8_e4m3fn_x4
 ACT = mybir.ActivationFunctionType
 ALU = mybir.AluOpType
 
-LOADS = (((0, 1024), (1024, 1024)), ((0, 1024), (1024, 768), (1792, 256)))
-PIECES = ((0, 256), (256, 256), (512, 256), (768, 256))
-WARM = 24
-PLAIN = {0: "S", 1: "G"}
+LOADS = (((0, 1024), (1024, 1024)),) * 3 + (((0, 1024), (1024, 768), (1792, 256)),)
+CASTS = ((("S", 0, 512), ("V", 512, 512), ("V", 1024, 1024)),) + ((("V", 0, 1024), ("V", 1024, 1024)),) * 2 + ((("V", 0, 1024), ("V", 1024, 768), ("V", 1792, 256)),)
+RUNS = (("V", 0, 384), ("S", 384, 384), ("S", 768, 256))
+QUANTS = ((0, 0, 512), (1, 0, 256), (1, 256, 128), (2, 0, 128), (2, 128, 128))
+PIECES = ((0, 0, 256), (0, 256, 128), (1, 0, 256), (2, 0, 128), (3, 0, 128), (4, 0, 128))
 
 
 def tile_picked_sub_lin_relu2_sub_e_kernel(tc, xT, w, b, gate, offs, pos1, pos2, pos3, out):
@@ -28,36 +28,30 @@ def tile_picked_sub_lin_relu2_sub_e_kernel(tc, xT, w, b, gate, offs, pos1, pos2,
         keep = ctx.enter_context(tc.tile_pool(name="keep", bufs=1))
         psum = ctx.enter_context(tc.psum_pool(name="psum", bufs=1))
 
-        raw = [[keep.tile([P, 2, n], F32, name=f"raw_{u}_{a}") for (a, n) in LOADS[u]] for u in range(2)]
-        pairs = [keep.tile([P, T, 2], BF16, name=f"pairs_{u}", align_bytes=64) for u in range(2)]
+        raw = [keep.tile([P, T], F32, name=f"raw_{j}") for j in range(4)]
+        rounded = [keep.tile([P, T], BF16, name=f"rounded_{j}", align_bytes=64) for j in range(4)]
         offsets = keep.tile([P, S // 16], U16, name="offsets")
         lists = [keep.tile([P, V // 16], U16, name=f"list_{d}") for d in range(D)]
         gates = [keep.tile([P, V], F32, name=f"gate_{d}") for d in range(D)]
         w_raw = keep.tile([P, 4, N], F32, name="w_raw")
-        w_grouped = keep.tile([P, N, 4], BF16, name="w_grouped", align_bytes=64)
-        w_codes = keep.tile([P, N], U32, name="w_codes", align_bytes=64)
-        w_scales = keep.tile([P, N], U8, name="w_scales", align_bytes=64)
         bias = keep.tile([P, 1], F32, name="bias")
-        grouped = [keep.tile([P, n, 4], BF16, name=f"grouped_{i}", align_bytes=64) for i, (a, n) in enumerate(PIECES)]
-        planar = {i: keep.tile([P, 2, PIECES[i][1]], U32, name=f"planar_{i}") for i in PLAIN}
-        codes = [keep.tile([P, n], U32, name=f"codes_{i}", align_bytes=64) for i, (a, n) in enumerate(PIECES)]
-        scales = [keep.tile([P, n], U8, name=f"scales_{i}", align_bytes=64) for i, (a, n) in enumerate(PIECES)]
-        rect = [keep.tile([P, n], F32, name=f"rect_{i}") for i, (a, n) in enumerate(PIECES)]
+        widths = [n + (N if r == 0 else 0) for r, (e, a, n) in enumerate(RUNS)]
+        grouped = [keep.tile([P, n, 4], BF16, name=f"grouped_{r}", align_bytes=64) for r, n in enumerate(widths)]
+        codes = [keep.tile([P, QUANTS[0][2]], U32, name="codes_0", align_bytes=64)[:]]
+        scales = [keep.tile([P, n], U8, name=f"scales_{q}", align_bytes=64) for q, (r, a, n) in enumerate(QUANTS)]
+        w_at = RUNS[0][2]
+        rect = [keep.tile([P, n], F32, name=f"rect_{i}") for i, (r, a, n) in enumerate(PIECES)]
         y = keep.tile([P, S], F32, name="y")
         turns = [keep.tile([P, V], F32, name=f"turn_{d}") for d in range(D)]
         partial = keep.tile([P, V], F32, name="partial")
         result = keep.tile([P, V], F32, name="result")
-        acc = [psum.tile([P, n], F32, name=f"acc_{i}") for i, (a, n) in enumerate(PIECES)]
+        acc = [psum.tile([P, n], F32, name=f"acc_{i}") for i, (r, a, n) in enumerate(PIECES)]
 
-        identity = keep.tile([P, P], BF16, name="identity", align_bytes=64)
-        make_identity(nc, identity[:])
-        warm = [psum.tile([P, 8, P], BF16, name=f"warm_{i}") for i in range(2)]
-
-        x_view = xT.rearrange("(p u j) t -> u p j t", u=2, j=2)
-        for u in range(2):
-            for c, (a, n) in enumerate(LOADS[u]):
-                nc.sync.dma_start(raw[u][c][:], x_view[u, :, :, a : a + n])
-            if u == 0:
+        x_view = xT.rearrange("(p j) t -> j p t", j=4)
+        for j in range(4):
+            for a, n in LOADS[j]:
+                nc.sync.dma_start(raw[j][:, a : a + n], x_view[j, :, a : a + n])
+            if j == 0:
                 nc.sync.dma_start(offsets[:], offs)
         nc.sync.dma_start(w_raw[:], w.rearrange("(p j) n -> p j n", j=4))
         nc.sync.dma_start(bias[:], b)
@@ -66,43 +60,39 @@ def tile_picked_sub_lin_relu2_sub_e_kernel(tc, xT, w, b, gate, offs, pos1, pos2,
         for d in range(D):
             nc.sync.dma_start(gates[d][:], gate[d])
 
-        def cast(engine, u, c, lo, hi):
-            a, n = LOADS[u][c]
-            dst = pairs[u][:, a + lo : a + hi, :]
-            src = raw[u][c][:, :, lo:hi].rearrange("p j t -> p t j")
+        def cast(engine, j, a, n):
+            dst, src = rounded[j][:, a : a + n], raw[j][:, a : a + n]
             if engine == "S":
                 nc.scalar.activation(dst, src, ACT.Copy)
+            elif engine == "G":
+                nc.gpsimd.tensor_scalar(dst, src, 1.0, 0.0, ALU.mult, ALU.add)
             else:
                 nc.vector.tensor_copy(dst, src)
 
-        def gather(u, i):
-            a, n = PIECES[i]
-            words = grouped[i][:].rearrange("p n k -> p (n k)").bitcast(U32).rearrange("p (n u) -> p n u", u=2)
-            window = pairs[u][:].rearrange("p t e -> p (t e)").bitcast(U32)
-            dst = planar[i][:, u, :] if i in PLAIN else words[:, :, u]
-            nc.vector.tensor_copy(dst, window.indirect(offsets[:, a // 16 : (a + n) // 16]))
-
-        def interleave(i):
-            src = planar[i][:].rearrange("p u n -> p (u n)").bitcast(BF16)
-            dst = grouped[i][:].rearrange("p n (u e) -> p n u e", u=2)
-            src = src.rearrange("p (u n e) -> p n u e", u=2, e=2)
-            if PLAIN[i] == "S":
-                nc.scalar.copy(dst, src)
+        def gather(j, r):
+            engine, a, n = RUNS[r]
+            picked = offsets[:, a // 16 : (a + n) // 16]
+            if engine == "S":
+                nc.scalar.activation(grouped[r][:, 0:n, j], rounded[j][:].indirect(picked), ACT.Copy)
             else:
-                nc.gpsimd.tensor_scalar(dst, src, 1.0, 0.0, ALU.mult, ALU.add)
+                nc.vector.tensor_copy(grouped[r][:, 0:n, j], raw[j][:].indirect(picked))
 
-        def quantize(i):
+        def quantize(q):
+            r, a, n = QUANTS[q]
             nc.vector.quantize_mx(
-                out=codes[i][:].bitcast(FP8X4), scales=scales[i][:], in_=grouped[i][:].rearrange("p n k -> p (n k)")
+                out=codes[q].bitcast(FP8X4),
+                scales=scales[q][:],
+                in_=grouped[r][:, a : a + n, :].rearrange("p n k -> p (n k)"),
             )
 
         def multiply(i):
+            q, a, n = PIECES[i]
             nc.tensor.matmul_mx(
                 out=acc[i][:],
-                lhsT=w_codes[:].bitcast(FP8X4),
-                lhsT_scale=w_scales[:],
-                rhs=codes[i][:].bitcast(FP8X4),
-                rhs_scale=scales[i][:],
+                lhsT=codes[0][:, w_at : w_at + N].bitcast(FP8X4),
+                lhsT_scale=scales[0][:, w_at : w_at + N],
+                rhs=codes[q][:, a : a + n].bitcast(FP8X4),
+                rhs_scale=scales[q][:, a : a + n],
                 start=True,
                 stop=True,
             )
@@ -114,48 +104,43 @@ def tile_picked_sub_lin_relu2_sub_e_kernel(tc, xT, w, b, gate, offs, pos1, pos2,
                 nc.vector.tensor_scalar(rect[i][:, lo:hi], acc[i][:, lo:hi], bias[:, 0:1], 0.0, ALU.add, ALU.max)
 
         def square(engine, i, lo, hi):
-            a, n = PIECES[i]
+            q, a, n = PIECES[i]
+            at = RUNS[QUANTS[q][0]][1] + QUANTS[q][1] + a
             if engine == "S":
-                nc.scalar.activation(y[:, a + lo : a + hi], rect[i][:, lo:hi], ACT.Square)
+                nc.scalar.activation(y[:, at + lo : at + hi], rect[i][:, lo:hi], ACT.Square)
             else:
-                nc.vector.tensor_tensor(y[:, a + lo : a + hi], rect[i][:, lo:hi], rect[i][:, lo:hi], ALU.mult)
+                nc.vector.tensor_tensor(y[:, at + lo : at + hi], rect[i][:, lo:hi], rect[i][:, lo:hi], ALU.mult)
 
-        cast("S", 0, 0, 0, 640)
-        cast("V", 0, 0, 640, 1024)
-        cast("S", 0, 1, 0, 352)
-        cast("V", 0, 1, 352, 1024)
-        for i in range(4):
-            gather(0, i)
-        cast("S", 1, 0, 0, 512)
-        cast("S", 1, 0, 512, 1024)
-        cast("V", 1, 1, 0, 640)
-        cast("S", 1, 1, 640, 768)
-        cast("V", 1, 2, 0, 176)
-        cast("S", 1, 2, 176, 256)
-        nc.gpsimd.tensor_scalar(w_grouped[:], w_raw[:].rearrange("p j n -> p n j"), 1.0, 0.0, ALU.mult, ALU.add)
-        last = pairs[1][:].rearrange("p t e -> p (t e)")
-        for i in range(WARM):
-            at = 2 * 1792 + (i % 4) * P
-            nc.tensor.transpose(warm[(i // 8) % 2][:, i % 8, :], last[:, at : at + P], identity[:])
-        for i in range(4):
-            gather(1, i)
-        interleave(0)
-        interleave(1)
-        nc.vector.quantize_mx(
-            out=w_codes[:].bitcast(FP8X4), scales=w_scales[:], in_=w_grouped[:].rearrange("p n j -> p (n j)")
+        for j in range(4):
+            for engine, a, n in CASTS[j]:
+                cast(engine, j, a, n)
+            for r in range(len(RUNS)):
+                gather(j, r)
+        nc.gpsimd.tensor_scalar(
+            grouped[0][:, w_at : w_at + N, :], w_raw[:].rearrange("p j n -> p n j"), 1.0, 0.0, ALU.mult, ALU.add
         )
-        for i in (2, 3, 0, 1):
-            quantize(i)
-            multiply(i)
-        relu("S", 2, 0, 256)
-        square("S", 2, 0, 256)
-        relu("S", 3, 0, 256)
-        square("S", 3, 0, 256)
-        relu("V", 0, 0, 256)
-        relu("V", 1, 0, 256)
+        for q in range(len(QUANTS)):
+            if q == 1:
+                later = keep.tile([P, S - w_at], U32, name="later_codes", tag="grouped_0", align_bytes=64)
+                for r, a, n in QUANTS[1:]:
+                    at = RUNS[r][1] + a - w_at
+                    codes.append(later[:, at : at + n])
+            quantize(q)
+            for i in range(len(PIECES)):
+                if PIECES[i][0] == q:
+                    multiply(i)
+        relu("S", 0, 0, 256)
+        relu("S", 1, 0, 128)
         square("S", 0, 0, 256)
-        square("V", 1, 0, 128)
-        square("S", 1, 128, 256)
+        relu("V", 2, 0, 256)
+        relu("V", 3, 0, 128)
+        square("S", 1, 0, 128)
+        relu("S", 4, 0, 128)
+        relu("V", 5, 0, 128)
+        square("V", 2, 0, 256)
+        square("S", 3, 0, 128)
+        square("S", 4, 0, 128)
+        square("V", 5, 0, 128)
 
         for d in range(D):
             nc.vector.tensor_tensor(turns[d][:], y[:].indirect(lists[d][:]), gates[d][:], ALU.mult)

@@ -1,6 +1,7 @@
 from contextlib import ExitStack
 
 import concourse.mybir as mybir
+from concourse.masks import make_identity
 
 K, T, D, S, V, N = 512, 2048, 3, 1024, 512, 128
 P = 128
@@ -16,10 +17,10 @@ ACT = mybir.ActivationFunctionType
 ALU = mybir.AluOpType
 
 LOADS = (((0, 1024), (1024, 1024)),) * 3 + (((0, 1024), (1024, 768), (1792, 256)),)
-CASTS = ((("S", 0, 512), ("V", 512, 512), ("V", 1024, 1024)),) + ((("V", 0, 1024), ("V", 1024, 1024)),) * 2 + ((("V", 0, 1024), ("V", 1024, 768), ("V", 1792, 256)),)
+CASTS = ((("S", 0, 512), ("V", 512, 512), ("V", 1024, 1024)),) + ((("G", 0, 576), ("V", 576, 448), ("V", 1024, 1024)),) * 2 + ((("G", 0, 576), ("V", 576, 448), ("V", 1024, 768), ("V", 1792, 256)),)
 RUNS = (("V", 0, 384), ("S", 384, 384), ("S", 768, 256))
-QUANTS = ((0, 0, 512), (1, 0, 256), (1, 256, 128), (2, 0, 128), (2, 128, 128))
-PIECES = ((0, 0, 256), (0, 256, 128), (1, 0, 256), (2, 0, 128), (3, 0, 128), (4, 0, 128))
+QUANTS = ((0, 0, 256), (0, 256, 256), (1, 0, 256), (1, 256, 128), (2, 0, 128), (2, 128, 128))
+PIECES = ((0, 128, 128), (1, 0, 256), (2, 0, 256), (3, 0, 128), (4, 0, 128), (5, 0, 128))
 
 
 def tile_picked_sub_lin_relu2_sub_e_kernel(tc, xT, w, b, gate, offs, pos1, pos2, pos3, out):
@@ -32,19 +33,21 @@ def tile_picked_sub_lin_relu2_sub_e_kernel(tc, xT, w, b, gate, offs, pos1, pos2,
         rounded = [keep.tile([P, T], BF16, name=f"rounded_{j}", align_bytes=64) for j in range(4)]
         offsets = keep.tile([P, S // 16], U16, name="offsets")
         lists = [keep.tile([P, V // 16], U16, name=f"list_{d}") for d in range(D)]
-        gates = [keep.tile([P, V], F32, name=f"gate_{d}") for d in range(D)]
+        gates = [keep.tile([P, D, V // 2], F32, name=f"gates_{h}") for h in range(2)]
         w_raw = keep.tile([P, 4, N], F32, name="w_raw")
         bias = keep.tile([P, 1], F32, name="bias")
         widths = [n + (N if r == 0 else 0) for r, (e, a, n) in enumerate(RUNS)]
         grouped = [keep.tile([P, n, 4], BF16, name=f"grouped_{r}", align_bytes=64) for r, n in enumerate(widths)]
-        codes = [keep.tile([P, QUANTS[0][2]], U32, name="codes_0", align_bytes=64)[:]]
+        codes = [keep.tile([P, QUANTS[q][2]], U32, name=f"codes_{q}", align_bytes=64)[:] for q in range(2)]
         scales = [keep.tile([P, n], U8, name=f"scales_{q}", align_bytes=64) for q, (r, a, n) in enumerate(QUANTS)]
-        w_at = RUNS[0][2]
+        lead = [N if r == 0 else 0 for r in range(len(RUNS))]
         rect = [keep.tile([P, n], F32, name=f"rect_{i}") for i, (r, a, n) in enumerate(PIECES)]
         y = keep.tile([P, S], F32, name="y")
-        turns = [keep.tile([P, V], F32, name=f"turn_{d}") for d in range(D)]
-        partial = keep.tile([P, V], F32, name="partial")
-        result = keep.tile([P, V], F32, name="result")
+        partial = keep.tile([P, V // 2], F32, name="partial")
+        result = keep.tile([P, V // 2], F32, name="result")
+        late = keep.tile([P, V // 2], F32, name="late")
+        identity = keep.tile([P, P], F32, name="identity")
+        make_identity(nc, identity[:])
         acc = [psum.tile([P, n], F32, name=f"acc_{i}") for i, (r, a, n) in enumerate(PIECES)]
 
         x_view = xT.rearrange("(p j) t -> j p t", j=4)
@@ -57,8 +60,8 @@ def tile_picked_sub_lin_relu2_sub_e_kernel(tc, xT, w, b, gate, offs, pos1, pos2,
         nc.sync.dma_start(bias[:], b)
         for d, pos in enumerate((pos1, pos2, pos3)):
             nc.sync.dma_start(lists[d][:], pos)
-        for d in range(D):
-            nc.sync.dma_start(gates[d][:], gate[d])
+        for h in range(2):
+            nc.sync.dma_start(gates[h][:], gate[:, :, h * 256 : (h + 1) * 256].rearrange("d p v -> p d v"))
 
         def cast(engine, j, a, n):
             dst, src = rounded[j][:, a : a + n], raw[j][:, a : a + n]
@@ -73,9 +76,9 @@ def tile_picked_sub_lin_relu2_sub_e_kernel(tc, xT, w, b, gate, offs, pos1, pos2,
             engine, a, n = RUNS[r]
             picked = offsets[:, a // 16 : (a + n) // 16]
             if engine == "S":
-                nc.scalar.activation(grouped[r][:, 0:n, j], rounded[j][:].indirect(picked), ACT.Copy)
+                nc.scalar.activation(grouped[r][:, lead[r] : lead[r] + n, j], rounded[j][:].indirect(picked), ACT.Copy)
             else:
-                nc.vector.tensor_copy(grouped[r][:, 0:n, j], raw[j][:].indirect(picked))
+                nc.vector.tensor_copy(grouped[r][:, lead[r] : lead[r] + n, j], raw[j][:].indirect(picked))
 
         def quantize(q):
             r, a, n = QUANTS[q]
@@ -89,8 +92,8 @@ def tile_picked_sub_lin_relu2_sub_e_kernel(tc, xT, w, b, gate, offs, pos1, pos2,
             q, a, n = PIECES[i]
             nc.tensor.matmul_mx(
                 out=acc[i][:],
-                lhsT=codes[0][:, w_at : w_at + N].bitcast(FP8X4),
-                lhsT_scale=scales[0][:, w_at : w_at + N],
+                lhsT=codes[0][:, 0:N].bitcast(FP8X4),
+                lhsT_scale=scales[0][:, 0:N],
                 rhs=codes[q][:, a : a + n].bitcast(FP8X4),
                 rhs_scale=scales[q][:, a : a + n],
                 start=True,
@@ -105,7 +108,8 @@ def tile_picked_sub_lin_relu2_sub_e_kernel(tc, xT, w, b, gate, offs, pos1, pos2,
 
         def square(engine, i, lo, hi):
             q, a, n = PIECES[i]
-            at = RUNS[QUANTS[q][0]][1] + QUANTS[q][1] + a
+            r = QUANTS[q][0]
+            at = RUNS[r][1] + QUANTS[q][1] + a - lead[r]
             if engine == "S":
                 nc.scalar.activation(y[:, at + lo : at + hi], rect[i][:, lo:hi], ACT.Square)
             else:
@@ -117,36 +121,63 @@ def tile_picked_sub_lin_relu2_sub_e_kernel(tc, xT, w, b, gate, offs, pos1, pos2,
             for r in range(len(RUNS)):
                 gather(j, r)
         nc.gpsimd.tensor_scalar(
-            grouped[0][:, w_at : w_at + N, :], w_raw[:].rearrange("p j n -> p n j"), 1.0, 0.0, ALU.mult, ALU.add
+            grouped[0][:, 0:N, :], w_raw[:].rearrange("p j n -> p n j"), 1.0, 0.0, ALU.mult, ALU.add
         )
         for q in range(len(QUANTS)):
-            if q == 1:
-                later = keep.tile([P, S - w_at], U32, name="later_codes", tag="grouped_0", align_bytes=64)
-                for r, a, n in QUANTS[1:]:
-                    at = RUNS[r][1] + a - w_at
+            if q == 2:
+                later = keep.tile([P, S - RUNS[0][2]], U32, name="later_codes", tag="grouped_0", align_bytes=64)
+                for r, a, n in QUANTS[2:]:
+                    at = RUNS[r][1] + a - RUNS[0][2]
                     codes.append(later[:, at : at + n])
             quantize(q)
             for i in range(len(PIECES)):
                 if PIECES[i][0] == q:
                     multiply(i)
-        relu("S", 0, 0, 256)
-        relu("S", 1, 0, 128)
-        square("S", 0, 0, 256)
+        relu("S", 0, 0, 128)
+        relu("S", 1, 0, 256)
+        square("S", 0, 0, 128)
         relu("V", 2, 0, 256)
+        square("S", 1, 0, 256)
         relu("V", 3, 0, 128)
-        square("S", 1, 0, 128)
         relu("S", 4, 0, 128)
         relu("V", 5, 0, 128)
-        square("V", 2, 0, 256)
-        square("S", 3, 0, 128)
-        square("S", 4, 0, 128)
+        square("S", 2, 0, 256)
+        square("V", 3, 0, 128)
         square("V", 5, 0, 128)
+        square("S", 4, 0, 128)
 
+        turns = [[keep.tile([P, V // 2], F32, name=f"turn_{h}_{d}") for d in range(D)] for h in range(2)]
+        for h in range(2):
+            for d in range(D):
+                nc.vector.tensor_tensor(
+                    turns[h][d][:],
+                    y[:].indirect(lists[d][:, h * 16 : (h + 1) * 16]),
+                    gates[h][:, d, :],
+                    ALU.mult,
+                )
+        summed = [psum.tile([P, P], F32, name=f"summed_{c}", tag=f"acc_{c}") for c in range(2)]
+        back = [psum.tile([P, P], F32, name=f"back_{c}", tag=f"acc_{2 + c}") for c in range(2)]
+        turned = [keep.tile([P, P], F32, name=f"turned_{c}") for c in range(2)]
         for d in range(D):
-            nc.vector.tensor_tensor(turns[d][:], y[:].indirect(lists[d][:]), gates[d][:], ALU.mult)
-        halves = (slice(0, 256), slice(256, 512))
-        for h in halves:
-            nc.vector.tensor_tensor(partial[:, h], turns[0][:, h], turns[1][:, h], ALU.add)
-        for h in halves:
-            nc.vector.tensor_tensor(result[:, h], partial[:, h], turns[2][:, h], ALU.add)
-            nc.sync.dma_start(out[:, h], result[:, h])
+            for c in range(2):
+                nc.tensor.matmul(
+                    summed[c][:],
+                    lhsT=turns[0][d][:, c * P : (c + 1) * P],
+                    rhs=identity[:],
+                    start=(d == 0),
+                    stop=(d == D - 1),
+                    is_transpose=True,
+                )
+        for c in range(2):
+            nc.scalar.copy(turned[c][:], summed[c][:])
+        for c in range(2):
+            nc.tensor.transpose(back[c][:], turned[c][:], identity[:])
+        for c in range(2):
+            nc.scalar.copy(result[:, c * P : (c + 1) * P], back[c][:])
+        nc.sync.dma_start(out[:, 0:256], result[:, 0:256])
+        quarters = (slice(0, 128), slice(128, 256))
+        for s in quarters:
+            nc.vector.tensor_tensor(partial[:, s], turns[1][0][:, s], turns[1][1][:, s], ALU.add)
+        for s in quarters:
+            nc.vector.tensor_tensor(late[:, s], partial[:, s], turns[1][2][:, s], ALU.add)
+        nc.sync.dma_start(out[:, 256:512], late[:])

@@ -17,10 +17,10 @@ ACT = mybir.ActivationFunctionType
 ALU = mybir.AluOpType
 
 LOADS = (((0, 1024), (1024, 1024)),) * 3 + (((0, 1024), (1024, 768), (1792, 256)),)
-CASTS = ((("S", 0, 512), ("V", 512, 512), ("V", 1024, 1024)),) + ((("G", 0, 576), ("V", 576, 448), ("V", 1024, 1024)),) * 2 + ((("G", 0, 576), ("V", 576, 448), ("V", 1024, 768), ("V", 1792, 256)),)
-RUNS = (("V", 0, 384), ("S", 384, 384), ("S", 768, 256))
-QUANTS = ((0, 0, 256), (0, 256, 256), (1, 0, 256), (1, 256, 128), (2, 0, 128), (2, 128, 128))
-PIECES = ((0, 128, 128), (1, 0, 256), (2, 0, 256), (3, 0, 128), (4, 0, 128), (5, 0, 128))
+CASTS = ((("S", 0, 512), ("V", 512, 512), ("V", 1024, 1024)),) + ((("G", 0, 1024), ("V", 1024, 1024)),) * 2 + ((("G", 0, 1024), ("V", 1024, 768), ("V", 1792, 256)),)
+GATHERS = ((("V", 0, 448), ("S", 448, 576)),) * 3 + ((("V", 0, 384), ("S", 384, 384), ("S", 768, 256)),)
+QUANTS = ((0, 256), (256, 256), (512, 256), (768, 128), (896, 128), (1024, 128))
+PIECES = ((0, 128), (128, 256), (384, 256), (640, 128), (768, 128), (896, 128))
 
 
 def tile_picked_sub_lin_relu2_sub_e_kernel(tc, xT, w, b, gate, offs, pos1, pos2, pos3, out):
@@ -34,21 +34,19 @@ def tile_picked_sub_lin_relu2_sub_e_kernel(tc, xT, w, b, gate, offs, pos1, pos2,
         offsets = keep.tile([P, S // 16], U16, name="offsets")
         lists = [keep.tile([P, V // 16], U16, name=f"list_{d}") for d in range(D)]
         gates = [keep.tile([P, D, V // 2], F32, name=f"gates_{h}") for h in range(2)]
-        w_raw = keep.tile([P, 4, N], F32, name="w_raw")
+        w_raw = keep.tile([P, 4, N], F32, name="w_raw", align_bytes=64)
         bias = keep.tile([P, 1], F32, name="bias")
-        widths = [n + (N if r == 0 else 0) for r, (e, a, n) in enumerate(RUNS)]
-        grouped = [keep.tile([P, n, 4], BF16, name=f"grouped_{r}", align_bytes=64) for r, n in enumerate(widths)]
-        codes = [keep.tile([P, QUANTS[q][2]], U32, name=f"codes_{q}", align_bytes=64)[:] for q in range(2)]
-        scales = [keep.tile([P, n], U8, name=f"scales_{q}", align_bytes=64) for q, (r, a, n) in enumerate(QUANTS)]
-        lead = [N if r == 0 else 0 for r in range(len(RUNS))]
-        rect = [keep.tile([P, n], F32, name=f"rect_{i}") for i, (r, a, n) in enumerate(PIECES)]
+        grouped = keep.tile([P, N + S, 4], BF16, name="grouped", align_bytes=64)
+        first_codes = keep.tile([P, QUANTS[0][1]], U32, name="first_codes", align_bytes=64)
+        scales = [keep.tile([P, n], U8, name=f"scales_{q}", align_bytes=64) for q, (a, n) in enumerate(QUANTS)]
+        rect = [keep.tile([P, n], F32, name=f"rect_{i}") for i, (a, n) in enumerate(PIECES)]
         y = keep.tile([P, S], F32, name="y")
         partial = keep.tile([P, V // 2], F32, name="partial")
         result = keep.tile([P, V // 2], F32, name="result")
         late = keep.tile([P, V // 2], F32, name="late")
         identity = keep.tile([P, P], F32, name="identity")
         make_identity(nc, identity[:])
-        acc = [psum.tile([P, n], F32, name=f"acc_{i}") for i, (r, a, n) in enumerate(PIECES)]
+        acc = [psum.tile([P, n], F32, name=f"acc_{i}") for i, (a, n) in enumerate(PIECES)]
 
         x_view = xT.rearrange("(p j) t -> j p t", j=4)
         for j in range(4):
@@ -72,30 +70,33 @@ def tile_picked_sub_lin_relu2_sub_e_kernel(tc, xT, w, b, gate, offs, pos1, pos2,
             else:
                 nc.vector.tensor_copy(dst, src)
 
-        def gather(j, r):
-            engine, a, n = RUNS[r]
+        def gather(engine, j, a, n):
             picked = offsets[:, a // 16 : (a + n) // 16]
+            dst = grouped[:, N + a : N + a + n, j]
             if engine == "S":
-                nc.scalar.activation(grouped[r][:, lead[r] : lead[r] + n, j], rounded[j][:].indirect(picked), ACT.Copy)
+                nc.scalar.activation(dst, rounded[j][:].indirect(picked), ACT.Copy)
             else:
-                nc.vector.tensor_copy(grouped[r][:, lead[r] : lead[r] + n, j], raw[j][:].indirect(picked))
+                nc.vector.tensor_copy(dst, raw[j][:].indirect(picked))
+
+        codes = [first_codes[:]]
 
         def quantize(q):
-            r, a, n = QUANTS[q]
+            a, n = QUANTS[q]
             nc.vector.quantize_mx(
                 out=codes[q].bitcast(FP8X4),
                 scales=scales[q][:],
-                in_=grouped[r][:, a : a + n, :].rearrange("p n k -> p (n k)"),
+                in_=grouped[:, a : a + n, :].rearrange("p n k -> p (n k)"),
             )
 
         def multiply(i):
-            q, a, n = PIECES[i]
+            lead = N if i == 0 else 0
+            n = PIECES[i][1]
             nc.tensor.matmul_mx(
                 out=acc[i][:],
                 lhsT=codes[0][:, 0:N].bitcast(FP8X4),
                 lhsT_scale=scales[0][:, 0:N],
-                rhs=codes[q][:, a : a + n].bitcast(FP8X4),
-                rhs_scale=scales[q][:, a : a + n],
+                rhs=codes[i][:, lead : lead + n].bitcast(FP8X4),
+                rhs_scale=scales[i][:, lead : lead + n],
                 start=True,
                 stop=True,
             )
@@ -107,9 +108,7 @@ def tile_picked_sub_lin_relu2_sub_e_kernel(tc, xT, w, b, gate, offs, pos1, pos2,
                 nc.vector.tensor_scalar(rect[i][:, lo:hi], acc[i][:, lo:hi], bias[:, 0:1], 0.0, ALU.add, ALU.max)
 
         def square(engine, i, lo, hi):
-            q, a, n = PIECES[i]
-            r = QUANTS[q][0]
-            at = RUNS[r][1] + QUANTS[q][1] + a - lead[r]
+            at = PIECES[i][0]
             if engine == "S":
                 nc.scalar.activation(y[:, at + lo : at + hi], rect[i][:, lo:hi], ACT.Square)
             else:
@@ -118,21 +117,17 @@ def tile_picked_sub_lin_relu2_sub_e_kernel(tc, xT, w, b, gate, offs, pos1, pos2,
         for j in range(4):
             for engine, a, n in CASTS[j]:
                 cast(engine, j, a, n)
-            for r in range(len(RUNS)):
-                gather(j, r)
+            for engine, a, n in GATHERS[j]:
+                gather(engine, j, a, n)
         nc.gpsimd.tensor_scalar(
-            grouped[0][:, 0:N, :], w_raw[:].rearrange("p j n -> p n j"), 1.0, 0.0, ALU.mult, ALU.add
+            grouped[:, 0:N, :], w_raw[:].rearrange("p j n -> p n j"), 1.0, 0.0, ALU.mult, ALU.add
         )
+        later = keep.tile([P, N + S - QUANTS[0][1]], U32, name="later_codes", tag="w_raw", align_bytes=64)
+        for a, n in QUANTS[1:]:
+            codes.append(later[:, a - QUANTS[0][1] : a - QUANTS[0][1] + n])
         for q in range(len(QUANTS)):
-            if q == 2:
-                later = keep.tile([P, S - RUNS[0][2]], U32, name="later_codes", tag="grouped_0", align_bytes=64)
-                for r, a, n in QUANTS[2:]:
-                    at = RUNS[r][1] + a - RUNS[0][2]
-                    codes.append(later[:, at : at + n])
             quantize(q)
-            for i in range(len(PIECES)):
-                if PIECES[i][0] == q:
-                    multiply(i)
+            multiply(q)
         relu("S", 0, 0, 128)
         relu("S", 1, 0, 256)
         square("S", 0, 0, 128)

@@ -16,11 +16,15 @@ FP8X4 = mybir.dt.float8_e4m3fn_x4
 ACT = mybir.ActivationFunctionType
 ALU = mybir.AluOpType
 
-LOADS = (((0, 1024), (1024, 1024)),) * 3 + (((0, 1024), (1024, 768), (1792, 256)),)
-CASTS = ((("S", 0, 512), ("V", 512, 512), ("V", 1024, 1024)),) + ((("G", 0, 1024), ("V", 1024, 1024)),) * 2 + ((("G", 0, 1024), ("V", 1024, 768), ("V", 1792, 256)),)
-GATHERS = ((("V", 0, 448), ("S", 448, 576)),) * 3 + ((("V", 0, 384), ("S", 384, 384), ("S", 768, 256)),)
-QUANTS = ((0, 256), (256, 256), (512, 256), (768, 128), (896, 128), (1024, 128))
-PIECES = ((0, 128), (128, 256), (384, 256), (640, 128), (768, 128), (896, 128))
+LOADS = (((0, 2048),),) + (((0, 1024), (1024, 1024)),) * 3
+CASTS = ((("S", 0, 1152), ("G", 1152, 896)),) + ((("G", 0, 1024), ("V", 1024, 1024)),) * 3
+GATHERS = (
+    (("V", 0, 576), ("S", 576, 448)),
+    (("V", 0, 448), ("S", 448, 576)),
+    (("V", 0, 448), ("S", 448, 576)),
+    (("V", 0, 384), ("S", 384, 384), ("S", 768, 256)),
+)
+PIECES = ((0, 256), (256, 256), (512, 256), (768, 128), (896, 128))
 
 
 def tile_picked_sub_lin_relu2_sub_e_kernel(tc, xT, w, b, gate, offs, pos1, pos2, pos3, out):
@@ -36,9 +40,11 @@ def tile_picked_sub_lin_relu2_sub_e_kernel(tc, xT, w, b, gate, offs, pos1, pos2,
         gates = [keep.tile([P, D, V // 2], F32, name=f"gates_{h}") for h in range(2)]
         w_raw = keep.tile([P, 4, N], F32, name="w_raw", align_bytes=64)
         bias = keep.tile([P, 1], F32, name="bias")
-        grouped = keep.tile([P, N + S, 4], BF16, name="grouped", align_bytes=64)
-        first_codes = keep.tile([P, QUANTS[0][1]], U32, name="first_codes", align_bytes=64)
-        scales = [keep.tile([P, n], U8, name=f"scales_{q}", align_bytes=64) for q, (a, n) in enumerate(QUANTS)]
+        grouped = keep.tile([P, S, 4], BF16, name="grouped", align_bytes=64)
+        w_grouped = keep.tile([P, N, 4], BF16, name="w_grouped", align_bytes=64)
+        w_codes = keep.tile([P, N], U32, name="w_codes", align_bytes=64)
+        w_scales = keep.tile([P, N], U8, name="w_scales", align_bytes=64)
+        scales = [keep.tile([P, n], U8, name=f"scales_{q}", align_bytes=64) for q, (a, n) in enumerate(PIECES)]
         rect = [keep.tile([P, n], F32, name=f"rect_{i}") for i, (a, n) in enumerate(PIECES)]
         y = keep.tile([P, S], F32, name="y")
         partial = keep.tile([P, V // 2], F32, name="partial")
@@ -72,31 +78,28 @@ def tile_picked_sub_lin_relu2_sub_e_kernel(tc, xT, w, b, gate, offs, pos1, pos2,
 
         def gather(engine, j, a, n):
             picked = offsets[:, a // 16 : (a + n) // 16]
-            dst = grouped[:, N + a : N + a + n, j]
+            dst = grouped[:, a : a + n, j]
             if engine == "S":
                 nc.scalar.activation(dst, rounded[j][:].indirect(picked), ACT.Copy)
             else:
                 nc.vector.tensor_copy(dst, raw[j][:].indirect(picked))
 
-        codes = [first_codes[:]]
-
-        def quantize(q):
-            a, n = QUANTS[q]
+        def quantize(i):
+            a, n = PIECES[i]
             nc.vector.quantize_mx(
-                out=codes[q].bitcast(FP8X4),
-                scales=scales[q][:],
+                out=codes[:, a : a + n].bitcast(FP8X4),
+                scales=scales[i][:],
                 in_=grouped[:, a : a + n, :].rearrange("p n k -> p (n k)"),
             )
 
         def multiply(i):
-            lead = N if i == 0 else 0
-            n = PIECES[i][1]
+            a, n = PIECES[i]
             nc.tensor.matmul_mx(
                 out=acc[i][:],
-                lhsT=codes[0][:, 0:N].bitcast(FP8X4),
-                lhsT_scale=scales[0][:, 0:N],
-                rhs=codes[i][:, lead : lead + n].bitcast(FP8X4),
-                rhs_scale=scales[i][:, lead : lead + n],
+                lhsT=w_codes[:].bitcast(FP8X4),
+                lhsT_scale=w_scales[:],
+                rhs=codes[:, a : a + n].bitcast(FP8X4),
+                rhs_scale=scales[i][:],
                 start=True,
                 stop=True,
             )
@@ -119,27 +122,24 @@ def tile_picked_sub_lin_relu2_sub_e_kernel(tc, xT, w, b, gate, offs, pos1, pos2,
                 cast(engine, j, a, n)
             for engine, a, n in GATHERS[j]:
                 gather(engine, j, a, n)
-        nc.gpsimd.tensor_scalar(
-            grouped[:, 0:N, :], w_raw[:].rearrange("p j n -> p n j"), 1.0, 0.0, ALU.mult, ALU.add
+        nc.gpsimd.tensor_scalar(w_grouped[:], w_raw[:].rearrange("p j n -> p n j"), 1.0, 0.0, ALU.mult, ALU.add)
+        codes = keep.tile([P, S], U32, name="codes", tag="w_raw", align_bytes=64)
+        nc.vector.quantize_mx(
+            out=w_codes[:].bitcast(FP8X4), scales=w_scales[:], in_=w_grouped[:].rearrange("p n k -> p (n k)")
         )
-        later = keep.tile([P, N + S - QUANTS[0][1]], U32, name="later_codes", tag="w_raw", align_bytes=64)
-        for a, n in QUANTS[1:]:
-            codes.append(later[:, a - QUANTS[0][1] : a - QUANTS[0][1] + n])
-        for q in range(len(QUANTS)):
-            quantize(q)
-            multiply(q)
-        relu("S", 0, 0, 128)
+        for i in range(len(PIECES)):
+            quantize(i)
+            multiply(i)
+        relu("S", 0, 0, 256)
         relu("S", 1, 0, 256)
-        square("S", 0, 0, 128)
         relu("V", 2, 0, 256)
-        square("S", 1, 0, 256)
+        square("S", 0, 0, 256)
         relu("V", 3, 0, 128)
         relu("S", 4, 0, 128)
-        relu("V", 5, 0, 128)
+        square("V", 1, 0, 256)
         square("S", 2, 0, 256)
-        square("V", 3, 0, 128)
-        square("V", 5, 0, 128)
-        square("S", 4, 0, 128)
+        square("V", 4, 0, 128)
+        square("S", 3, 0, 128)
 
         turns = [[keep.tile([P, V // 2], F32, name=f"turn_{h}_{d}") for d in range(D)] for h in range(2)]
         for h in range(2):

@@ -16,13 +16,18 @@ FP8X4 = mybir.dt.float8_e4m3fn_x4
 ACT = mybir.ActivationFunctionType
 ALU = mybir.AluOpType
 
-LOADS = (((0, 2048),),) + (((0, 1024), (1024, 1024)),) * 3
-CASTS = ((("S", 0, 1152), ("G", 1152, 896)),) + ((("G", 0, 1024), ("V", 1024, 1024)),) * 3
+LOADS = (((0, 2048),),) + (((0, 1024), (1024, 1024)),) * 2 + (((0, 896), (896, 768), (1664, 384)),)
+CASTS = (
+    (("S", 0, 1152), ("G", 1152, 896)),
+    (("G", 0, 1024), ("V", 1024, 1024)),
+    (("G", 0, 1024), ("V", 1024, 1024)),
+    (("G", 0, 896), ("V", 896, 768), ("V", 1664, 384)),
+)
 GATHERS = (
     (("V", 0, 576), ("S", 576, 448)),
     (("V", 0, 448), ("S", 448, 576)),
     (("V", 0, 448), ("S", 448, 576)),
-    (("V", 0, 384), ("S", 384, 384), ("S", 768, 256)),
+    (("V", 0, 416), ("S", 416, 352), ("S", 768, 256)),
 )
 PIECES = ((0, 256), (256, 256), (512, 256), (768, 128), (896, 128))
 
@@ -169,10 +174,10 @@ def tile_picked_sub_lin_relu2_sub_e_kernel(tc, xT, w, b, gate, offs, pos1, pos2,
             nc.tensor.transpose(back[c][:], turned[c][:], identity[:])
         for c in range(2):
             nc.scalar.copy(result[:, c * P : (c + 1) * P], back[c][:])
-        nc.sync.dma_start(out[:, 0:256], result[:, 0:256])
+        nc.scalar.dma_start(out[:, 0:256], result[:, 0:256])
         quarters = (slice(0, 128), slice(128, 256))
         for s in quarters:
             nc.vector.tensor_tensor(partial[:, s], turns[1][0][:, s], turns[1][1][:, s], ALU.add)
         for s in quarters:
             nc.vector.tensor_tensor(late[:, s], partial[:, s], turns[1][2][:, s], ALU.add)
-        nc.sync.dma_start(out[:, 256:512], late[:])
+            nc.sync.dma_start(out[:, 256 + s.start : 256 + s.stop], late[:, s])

@@ -27,7 +27,7 @@ GATHERS = (
     (("V", 0, 576), ("S", 576, 448)),
     (("V", 0, 448), ("S", 448, 576)),
     (("V", 0, 448), ("S", 448, 576)),
-    (("V", 0, 416), ("S", 416, 352), ("S", 768, 256)),
+    (("V", 0, 384), ("S", 384, 384), ("S", 768, 256)),
 )
 PIECES = ((0, 256), (256, 256), (512, 256), (768, 128), (896, 128))
 
@@ -137,14 +137,14 @@ def tile_picked_sub_lin_relu2_sub_e_kernel(tc, xT, w, b, gate, offs, pos1, pos2,
             multiply(i)
         relu("S", 0, 0, 256)
         relu("S", 1, 0, 256)
-        relu("V", 2, 0, 256)
-        square("S", 0, 0, 256)
+        square("V", 0, 0, 256)
+        relu("S", 2, 0, 256)
         relu("V", 3, 0, 128)
-        relu("S", 4, 0, 128)
-        square("V", 1, 0, 256)
-        square("S", 2, 0, 256)
-        square("V", 4, 0, 128)
+        relu("V", 4, 0, 128)
+        square("S", 1, 0, 256)
+        square("V", 2, 0, 256)
         square("S", 3, 0, 128)
+        square("S", 4, 0, 128)
 
         turns = [[keep.tile([P, V // 2], F32, name=f"turn_{h}_{d}") for d in range(D)] for h in range(2)]
         for h in range(2):

@@ -27,7 +27,7 @@ GATHERS = (
     (("V", 0, 576), ("S", 576, 448)),
     (("V", 0, 448), ("S", 448, 576)),
     (("V", 0, 448), ("S", 448, 576)),
-    (("V", 0, 384), ("S", 384, 384), ("S", 768, 256)),
+    (("V", 0, 448), ("S", 448, 320), ("S", 768, 256)),
 )
 PIECES = ((0, 256), (256, 256), (512, 256), (768, 128), (896, 128))
 
@@ -174,10 +174,10 @@ def tile_picked_sub_lin_relu2_sub_e_kernel(tc, xT, w, b, gate, offs, pos1, pos2,
             nc.tensor.transpose(back[c][:], turned[c][:], identity[:])
         for c in range(2):
             nc.scalar.copy(result[:, c * P : (c + 1) * P], back[c][:])
-        nc.scalar.dma_start(out[:, 0:256], result[:, 0:256])
+        nc.sync.dma_start(out[:, 0:256], result[:, 0:256])
         quarters = (slice(0, 128), slice(128, 256))
         for s in quarters:
             nc.vector.tensor_tensor(partial[:, s], turns[1][0][:, s], turns[1][1][:, s], ALU.add)
         for s in quarters:
             nc.vector.tensor_tensor(late[:, s], partial[:, s], turns[1][2][:, s], ALU.add)
-            nc.sync.dma_start(out[:, 256 + s.start : 256 + s.stop], late[:, s])
+        nc.sync.dma_start(out[:, 256:512], late[:])

@@ -1,7 +1,6 @@
 from contextlib import ExitStack
 
 import concourse.mybir as mybir
-from concourse.masks import make_identity
 
 K, T, D, S, V, N = 512, 2048, 3, 1024, 512, 128
 P = 128
@@ -42,7 +41,7 @@ def tile_picked_sub_lin_relu2_sub_e_kernel(tc, xT, w, b, gate, offs, pos1, pos2,
         rounded = [keep.tile([P, T], BF16, name=f"rounded_{j}", align_bytes=64) for j in range(4)]
         offsets = keep.tile([P, S // 16], U16, name="offsets")
         lists = [keep.tile([P, V // 16], U16, name=f"list_{d}") for d in range(D)]
-        gates = [keep.tile([P, D, V // 2], F32, name=f"gates_{h}") for h in range(2)]
+        gates = keep.tile([P, D, V], F32, name="gates")
         w_raw = keep.tile([P, 4, N], F32, name="w_raw", align_bytes=64)
         bias = keep.tile([P, 1], F32, name="bias")
         grouped = keep.tile([P, S, 4], BF16, name="grouped", align_bytes=64)
@@ -52,11 +51,10 @@ def tile_picked_sub_lin_relu2_sub_e_kernel(tc, xT, w, b, gate, offs, pos1, pos2,
         scales = [keep.tile([P, n], U8, name=f"scales_{q}", align_bytes=64) for q, (a, n) in enumerate(PIECES)]
         rect = [keep.tile([P, n], F32, name=f"rect_{i}") for i, (a, n) in enumerate(PIECES)]
         y = keep.tile([P, S], F32, name="y")
-        partial = keep.tile([P, V // 2], F32, name="partial")
-        result = keep.tile([P, V // 2], F32, name="result")
-        late = keep.tile([P, V // 2], F32, name="late")
-        identity = keep.tile([P, P], F32, name="identity")
-        make_identity(nc, identity[:])
+        fetched = keep.tile([P, D, V], F32, name="fetched")
+        weighted = keep.tile([P, D, V], F32, name="weighted")
+        partial = keep.tile([P, V], F32, name="partial")
+        result = keep.tile([P, V], F32, name="result")
         acc = [psum.tile([P, n], F32, name=f"acc_{i}") for i, (a, n) in enumerate(PIECES)]
 
         x_view = xT.rearrange("(p j) t -> j p t", j=4)
@@ -69,8 +67,7 @@ def tile_picked_sub_lin_relu2_sub_e_kernel(tc, xT, w, b, gate, offs, pos1, pos2,
         nc.sync.dma_start(bias[:], b)
         for d, pos in enumerate((pos1, pos2, pos3)):
             nc.sync.dma_start(lists[d][:], pos)
-        for h in range(2):
-            nc.sync.dma_start(gates[h][:], gate[:, :, h * 256 : (h + 1) * 256].rearrange("d p v -> p d v"))
+        nc.sync.dma_start(gates[:], gate.rearrange("d p v -> p d v"))
 
         def cast(engine, j, a, n):
             dst, src = rounded[j][:, a : a + n], raw[j][:, a : a + n]
@@ -146,38 +143,45 @@ def tile_picked_sub_lin_relu2_sub_e_kernel(tc, xT, w, b, gate, offs, pos1, pos2,
         square("S", 3, 0, 128)
         square("S", 4, 0, 128)
 
-        turns = [[keep.tile([P, V // 2], F32, name=f"turn_{h}_{d}") for d in range(D)] for h in range(2)]
-        for h in range(2):
-            for d in range(D):
-                nc.vector.tensor_tensor(
-                    turns[h][d][:],
-                    y[:].indirect(lists[d][:, h * 16 : (h + 1) * 16]),
-                    gates[h][:, d, :],
-                    ALU.mult,
-                )
-        summed = [psum.tile([P, P], F32, name=f"summed_{c}", tag=f"acc_{c}") for c in range(2)]
-        back = [psum.tile([P, P], F32, name=f"back_{c}", tag=f"acc_{2 + c}") for c in range(2)]
-        turned = [keep.tile([P, P], F32, name=f"turned_{c}") for c in range(2)]
-        for d in range(D):
-            for c in range(2):
-                nc.tensor.matmul(
-                    summed[c][:],
-                    lhsT=turns[0][d][:, c * P : (c + 1) * P],
-                    rhs=identity[:],
-                    start=(d == 0),
-                    stop=(d == D - 1),
-                    is_transpose=True,
-                )
-        for c in range(2):
-            nc.scalar.copy(turned[c][:], summed[c][:])
-        for c in range(2):
-            nc.tensor.transpose(back[c][:], turned[c][:], identity[:])
-        for c in range(2):
-            nc.scalar.copy(result[:, c * P : (c + 1) * P], back[c][:])
-        nc.sync.dma_start(out[:, 0:256], result[:, 0:256])
-        quarters = (slice(0, 128), slice(128, 256))
-        for s in quarters:
-            nc.vector.tensor_tensor(partial[:, s], turns[1][0][:, s], turns[1][1][:, s], ALU.add)
-        for s in quarters:
-            nc.vector.tensor_tensor(late[:, s], partial[:, s], turns[1][2][:, s], ALU.add)
-        nc.sync.dma_start(out[:, 256:512], late[:])
+        def fetch(d, lo, hi):
+            nc.scalar.activation(fetched[:, d, lo:hi], y[:].indirect(lists[d][:, lo // 16 : hi // 16]), ACT.Copy)
+
+        def fetch_weighted(d, lo, hi):
+            nc.vector.tensor_tensor(
+                weighted[:, d, lo:hi], y[:].indirect(lists[d][:, lo // 16 : hi // 16]), gates[:, d, lo:hi], ALU.mult
+            )
+
+        def weigh(d0, d1, lo, hi):
+            nc.vector.tensor_tensor(weighted[:, d0:d1, lo:hi], fetched[:, d0:d1, lo:hi], gates[:, d0:d1, lo:hi], ALU.mult)
+
+        def add_first(lo, hi):
+            nc.vector.tensor_tensor(partial[:, lo:hi], weighted[:, 0, lo:hi], weighted[:, 1, lo:hi], ALU.add)
+
+        def add_last(lo, hi):
+            nc.vector.tensor_tensor(result[:, lo:hi], partial[:, lo:hi], weighted[:, 2, lo:hi], ALU.add)
+
+        def store(lo, hi):
+            nc.sync.dma_start(out[:, lo:hi], result[:, lo:hi])
+
+        fetch(1, 0, 256)
+        fetch(2, 0, 256)
+        fetch(1, 256, 384)
+        fetch(2, 256, 384)
+        fetch(0, 384, 512)
+        fetch(1, 384, 512)
+        fetch(2, 384, 512)
+        fetch_weighted(0, 0, 256)
+        fetch_weighted(0, 256, 384)
+        weigh(1, 2, 0, 256)
+        weigh(2, 3, 0, 256)
+        add_first(0, 256)
+        weigh(1, 3, 256, 384)
+        add_last(0, 256)
+        store(0, 256)
+        add_first(256, 384)
+        weigh(0, 2, 384, 512)
+        add_last(256, 384)
+        weigh(2, 3, 384, 512)
+        add_first(384, 512)
+        add_last(384, 512)
+        store(256, 512)

@@ -1,6 +1,7 @@
 from contextlib import ExitStack
 
 import concourse.mybir as mybir
+from concourse.masks import make_identity
 
 K, T, D, S, V, N = 512, 2048, 3, 1024, 512, 128
 P = 128
@@ -15,19 +16,8 @@ FP8X4 = mybir.dt.float8_e4m3fn_x4
 ACT = mybir.ActivationFunctionType
 ALU = mybir.AluOpType
 
-LOADS = (((0, 2048),),) + (((0, 1024), (1024, 1024)),) * 2 + (((0, 896), (896, 768), (1664, 384)),)
-CASTS = (
-    (("S", 0, 1152), ("G", 1152, 896)),
-    (("G", 0, 1024), ("V", 1024, 1024)),
-    (("G", 0, 1024), ("V", 1024, 1024)),
-    (("G", 0, 896), ("V", 896, 768), ("V", 1664, 384)),
-)
-GATHERS = (
-    (("V", 0, 576), ("S", 576, 448)),
-    (("V", 0, 448), ("S", 448, 576)),
-    (("V", 0, 448), ("S", 448, 576)),
-    (("V", 0, 448), ("S", 448, 320), ("S", 768, 256)),
-)
+DIRECT = 448
+RUNS = ((448, 192, "VV"), (640, 128, "VS"), (768, 256, "VS"))
 PIECES = ((0, 256), (256, 256), (512, 256), (768, 128), (896, 128))
 
 
@@ -38,12 +28,20 @@ def tile_picked_sub_lin_relu2_sub_e_kernel(tc, xT, w, b, gate, offs, pos1, pos2,
         psum = ctx.enter_context(tc.psum_pool(name="psum", bufs=1))
 
         raw = [keep.tile([P, T], F32, name=f"raw_{j}") for j in range(4)]
-        rounded = [keep.tile([P, T], BF16, name=f"rounded_{j}", align_bytes=64) for j in range(4)]
         offsets = keep.tile([P, S // 16], U16, name="offsets")
         lists = [keep.tile([P, V // 16], U16, name=f"list_{d}") for d in range(D)]
-        gates = keep.tile([P, D, V], F32, name="gates")
+        gate_first = keep.tile([P, V], F32, name="gate_first")
+        gate_rest = keep.tile([P, 2, 256], F32, name="gate_rest")
+        gate_turned = [keep.tile([P, 2], F32, name=f"gate_turned_{d}") for d in (1, 2)]
+        identity = keep.tile([P, P], F32, name="identity")
+        make_identity(nc, identity[:])
         w_raw = keep.tile([P, 4, N], F32, name="w_raw", align_bytes=64)
         bias = keep.tile([P, 1], F32, name="bias")
+        floor = keep.tile([P, 1], F32, name="floor")
+        rows = [
+            [keep.tile([P, 2, n], BF16, name=f"rows_{u}_{r}", align_bytes=64) for r, (a, n, who) in enumerate(RUNS)]
+            for u in range(2)
+        ]
         grouped = keep.tile([P, S, 4], BF16, name="grouped", align_bytes=64)
         w_grouped = keep.tile([P, N, 4], BF16, name="w_grouped", align_bytes=64)
         w_codes = keep.tile([P, N], U32, name="w_codes", align_bytes=64)
@@ -51,40 +49,49 @@ def tile_picked_sub_lin_relu2_sub_e_kernel(tc, xT, w, b, gate, offs, pos1, pos2,
         scales = [keep.tile([P, n], U8, name=f"scales_{q}", align_bytes=64) for q, (a, n) in enumerate(PIECES)]
         rect = [keep.tile([P, n], F32, name=f"rect_{i}") for i, (a, n) in enumerate(PIECES)]
         y = keep.tile([P, S], F32, name="y")
-        fetched = keep.tile([P, D, V], F32, name="fetched")
-        weighted = keep.tile([P, D, V], F32, name="weighted")
         partial = keep.tile([P, V], F32, name="partial")
         result = keep.tile([P, V], F32, name="result")
         acc = [psum.tile([P, n], F32, name=f"acc_{i}") for i, (a, n) in enumerate(PIECES)]
 
+        nc.scalar.dma_start(bias[:], b)
+        nc.scalar.mul(floor[:], bias[:], -1.0)
         x_view = xT.rearrange("(p j) t -> j p t", j=4)
         for j in range(4):
-            for a, n in LOADS[j]:
-                nc.sync.dma_start(raw[j][:, a : a + n], x_view[j, :, a : a + n])
+            nc.sync.dma_start(raw[j][:], x_view[j])
             if j == 0:
                 nc.sync.dma_start(offsets[:], offs)
         nc.sync.dma_start(w_raw[:], w.rearrange("(p j) n -> p j n", j=4))
-        nc.sync.dma_start(bias[:], b)
         for d, pos in enumerate((pos1, pos2, pos3)):
             nc.sync.dma_start(lists[d][:], pos)
-        nc.sync.dma_start(gates[:], gate.rearrange("d p v -> p d v"))
+        nc.sync.dma_start(gate_first[:], gate[0])
+        nc.sync.dma_start(gate_rest[:], gate[1:3, :, 256:512].rearrange("d p v -> p d v"))
+        with nc.allow_non_contiguous_dma(reason="one gate value a partition"):
+            for d in (1, 2):
+                nc.sync.dma_start(gate_turned[d - 1][:], gate[d, 0, 0:256].rearrange("(c p) -> p c", p=P))
 
-        def cast(engine, j, a, n):
-            dst, src = rounded[j][:, a : a + n], raw[j][:, a : a + n]
-            if engine == "S":
-                nc.scalar.activation(dst, src, ACT.Copy)
-            elif engine == "G":
+        def window(j, a, n):
+            return raw[j][:].indirect(offsets[:, a // 16 : (a + n) // 16])
+
+        def move(who, dst, src):
+            if who == "S":
+                nc.scalar.copy(dst, src)
+            elif who == "G":
                 nc.gpsimd.tensor_scalar(dst, src, 1.0, 0.0, ALU.mult, ALU.add)
             else:
                 nc.vector.tensor_copy(dst, src)
 
-        def gather(engine, j, a, n):
-            picked = offsets[:, a // 16 : (a + n) // 16]
-            dst = grouped[:, a : a + n, j]
-            if engine == "S":
-                nc.scalar.activation(dst, rounded[j][:].indirect(picked), ACT.Copy)
-            else:
-                nc.vector.tensor_copy(dst, raw[j][:].indirect(picked))
+        def gather(j, r):
+            a, n, who = RUNS[r]
+            nc.scalar.activation(rows[j // 2][r][:, j % 2, :], window(j, a, n), ACT.Copy)
+
+        def place(u, r):
+            a, n, who = RUNS[r]
+            move(who[u], grouped[:, a : a + n, 2 * u : 2 * u + 2], rows[u][r][:].rearrange("p j n -> p n j"))
+
+        def quantize_w():
+            nc.vector.quantize_mx(
+                out=w_codes[:].bitcast(FP8X4), scales=w_scales[:], in_=w_grouped[:].rearrange("p n k -> p (n k)")
+            )
 
         def quantize(i):
             a, n = PIECES[i]
@@ -93,9 +100,6 @@ def tile_picked_sub_lin_relu2_sub_e_kernel(tc, xT, w, b, gate, offs, pos1, pos2,
                 scales=scales[i][:],
                 in_=grouped[:, a : a + n, :].rearrange("p n k -> p (n k)"),
             )
-
-        def multiply(i):
-            a, n = PIECES[i]
             nc.tensor.matmul_mx(
                 out=acc[i][:],
                 lhsT=w_codes[:].bitcast(FP8X4),
@@ -110,7 +114,7 @@ def tile_picked_sub_lin_relu2_sub_e_kernel(tc, xT, w, b, gate, offs, pos1, pos2,
             if engine == "S":
                 nc.scalar.activation(rect[i][:, lo:hi], acc[i][:, lo:hi], ACT.Relu, bias=bias[:, 0:1])
             else:
-                nc.vector.tensor_scalar(rect[i][:, lo:hi], acc[i][:, lo:hi], bias[:, 0:1], 0.0, ALU.add, ALU.max)
+                nc.vector.tensor_scalar(rect[i][:, lo:hi], acc[i][:, lo:hi], floor[:, 0:1], bias[:, 0:1], ALU.max, ALU.add)
 
         def square(engine, i, lo, hi):
             at = PIECES[i][0]
@@ -119,19 +123,24 @@ def tile_picked_sub_lin_relu2_sub_e_kernel(tc, xT, w, b, gate, offs, pos1, pos2,
             else:
                 nc.vector.tensor_tensor(y[:, at + lo : at + hi], rect[i][:, lo:hi], rect[i][:, lo:hi], ALU.mult)
 
-        for j in range(4):
-            for engine, a, n in CASTS[j]:
-                cast(engine, j, a, n)
-            for engine, a, n in GATHERS[j]:
-                gather(engine, j, a, n)
-        nc.gpsimd.tensor_scalar(w_grouped[:], w_raw[:].rearrange("p j n -> p n j"), 1.0, 0.0, ALU.mult, ALU.add)
+        w_turned = w_raw[:].rearrange("p j n -> p n j")
+        for j in range(3):
+            nc.vector.tensor_copy(grouped[:, 0:DIRECT, j], window(j, 0, DIRECT))
+            for r in range(len(RUNS)):
+                gather(j, r)
+            if j == 1:
+                for r in range(len(RUNS)):
+                    place(0, r)
+        nc.vector.tensor_copy(grouped[:, 0:DIRECT, 3], window(3, 0, DIRECT))
+        for r in range(len(RUNS)):
+            gather(3, r)
+        move("G", w_grouped[:], w_turned)
+        for r in range(len(RUNS)):
+            place(1, r)
         codes = keep.tile([P, S], U32, name="codes", tag="w_raw", align_bytes=64)
-        nc.vector.quantize_mx(
-            out=w_codes[:].bitcast(FP8X4), scales=w_scales[:], in_=w_grouped[:].rearrange("p n k -> p (n k)")
-        )
+        quantize_w()
         for i in range(len(PIECES)):
             quantize(i)
-            multiply(i)
         relu("S", 0, 0, 256)
         relu("S", 1, 0, 256)
         square("V", 0, 0, 256)
@@ -143,45 +152,48 @@ def tile_picked_sub_lin_relu2_sub_e_kernel(tc, xT, w, b, gate, offs, pos1, pos2,
         square("S", 3, 0, 128)
         square("S", 4, 0, 128)
 
-        def fetch(d, lo, hi):
-            nc.scalar.activation(fetched[:, d, lo:hi], y[:].indirect(lists[d][:, lo // 16 : hi // 16]), ACT.Copy)
-
-        def fetch_weighted(d, lo, hi):
-            nc.vector.tensor_tensor(
-                weighted[:, d, lo:hi], y[:].indirect(lists[d][:, lo // 16 : hi // 16]), gates[:, d, lo:hi], ALU.mult
-            )
-
-        def weigh(d0, d1, lo, hi):
-            nc.vector.tensor_tensor(weighted[:, d0:d1, lo:hi], fetched[:, d0:d1, lo:hi], gates[:, d0:d1, lo:hi], ALU.mult)
-
-        def add_first(lo, hi):
-            nc.vector.tensor_tensor(partial[:, lo:hi], weighted[:, 0, lo:hi], weighted[:, 1, lo:hi], ALU.add)
-
-        def add_last(lo, hi):
-            nc.vector.tensor_tensor(result[:, lo:hi], partial[:, lo:hi], weighted[:, 2, lo:hi], ALU.add)
-
         def store(lo, hi):
             nc.sync.dma_start(out[:, lo:hi], result[:, lo:hi])
 
-        fetch(1, 0, 256)
-        fetch(2, 0, 256)
-        fetch(1, 256, 384)
-        fetch(2, 256, 384)
-        fetch(0, 384, 512)
-        fetch(1, 384, 512)
-        fetch(2, 384, 512)
-        fetch_weighted(0, 0, 256)
-        fetch_weighted(0, 256, 384)
-        weigh(1, 2, 0, 256)
-        weigh(2, 3, 0, 256)
-        add_first(0, 256)
-        weigh(1, 3, 256, 384)
-        add_last(0, 256)
-        store(0, 256)
-        add_first(256, 384)
-        weigh(0, 2, 384, 512)
-        add_last(256, 384)
-        weigh(2, 3, 384, 512)
-        add_first(384, 512)
-        add_last(384, 512)
+        def picked(d, lo, hi):
+            return y[:].indirect(lists[d][:, lo // 16 : hi // 16])
+
+        got_a = [keep.tile([P, 256], F32, name=f"got_a_{d}") for d in (1, 2)]
+        got_b = keep.tile([P, 256], F32, name="got_b")
+        first = keep.tile([P, V], F32, name="first")
+        second = keep.tile([P, 256], F32, name="second")
+        third = keep.tile([P, 256], F32, name="third")
+        scaled = [keep.tile([P, 256], F32, name=f"scaled_{d}") for d in (1, 2)]
+        turned = [psum.tile([P, 256], F32, name=f"turned_{d}", tag=f"acc_{d - 1}") for d in (1, 2)]
+        back = [psum.tile([P, P], F32, name=f"back_{c}", tag=f"acc_{2 + c}") for c in range(2)]
+        for d in (1, 2):
+            nc.scalar.activation(got_a[d - 1][:], picked(d, 0, 256), ACT.Copy)
+            for c in range(2):
+                nc.tensor.transpose(turned[d - 1][:, c * P : (c + 1) * P], got_a[d - 1][:, c * P : (c + 1) * P], identity[:])
+        nc.scalar.activation(got_b[:], picked(2, 256, 512), ACT.Copy)
+        for d in (1, 2):
+            for c in range(2):
+                nc.scalar.activation(
+                    scaled[d - 1][:, c * P : (c + 1) * P],
+                    turned[d - 1][:, c * P : (c + 1) * P],
+                    ACT.Copy,
+                    scale=gate_turned[d - 1][:, c : c + 1],
+                )
+                nc.tensor.matmul(
+                    back[c][:],
+                    lhsT=scaled[d - 1][:, c * P : (c + 1) * P],
+                    rhs=identity[:],
+                    start=(d == 1),
+                    stop=(d == 2),
+                    is_transpose=True,
+                )
+        nc.vector.tensor_tensor(first[:, 256:512], picked(0, 256, 512), gate_first[:, 256:512], ALU.mult)
+        nc.vector.tensor_tensor(second[:], picked(1, 256, 512), gate_rest[:, 0, :], ALU.mult)
+        nc.vector.tensor_tensor(first[:, 0:256], picked(0, 0, 256), gate_first[:, 0:256], ALU.mult)
+        nc.vector.tensor_tensor(partial[:, 256:512], first[:, 256:512], second[:], ALU.add)
+        nc.vector.tensor_tensor(third[:], got_b[:], gate_rest[:, 1, :], ALU.mult)
+        nc.vector.tensor_tensor(result[:, 0:128], first[:, 0:128], back[0][:], ALU.add)
+        nc.vector.tensor_tensor(result[:, 256:512], partial[:, 256:512], third[:], ALU.add)
         store(256, 512)
+        nc.vector.tensor_tensor(result[:, 128:256], first[:, 128:256], back[1][:], ALU.add)
+        store(0, 256)

@@ -17,6 +17,7 @@ ACT = mybir.ActivationFunctionType
 ALU = mybir.AluOpType
 
 DIRECT = 448
+EARLY = 544
 RUNS = ((448, 192, "VV"), (640, 128, "VS"), (768, 256, "VS"))
 PIECES = ((0, 256), (256, 256), (512, 256), (768, 128), (896, 128))
 
@@ -37,30 +38,25 @@ def tile_picked_sub_lin_relu2_sub_e_kernel(tc, xT, w, b, gate, offs, pos1, pos2,
         make_identity(nc, identity[:])
         w_raw = keep.tile([P, 4, N], F32, name="w_raw", align_bytes=64)
         bias = keep.tile([P, 1], F32, name="bias")
-        floor = keep.tile([P, 1], F32, name="floor")
-        rows = [
-            [keep.tile([P, 2, n], BF16, name=f"rows_{u}_{r}", align_bytes=64) for r, (a, n, who) in enumerate(RUNS)]
-            for u in range(2)
-        ]
-        grouped = keep.tile([P, S, 4], BF16, name="grouped", align_bytes=64)
-        w_grouped = keep.tile([P, N, 4], BF16, name="w_grouped", align_bytes=64)
-        w_codes = keep.tile([P, N], U32, name="w_codes", align_bytes=64)
-        w_scales = keep.tile([P, N], U8, name="w_scales", align_bytes=64)
-        scales = [keep.tile([P, n], U8, name=f"scales_{q}", align_bytes=64) for q, (a, n) in enumerate(PIECES)]
+        early = keep.tile([P, 2, S - EARLY], BF16, name="early", align_bytes=64)
+        rows = [keep.tile([P, 2, n], BF16, name=f"rows_{r}", align_bytes=64) for r, (a, n, who) in enumerate(RUNS)]
+        columns = keep.tile([P, N + S, 4], BF16, name="columns", align_bytes=64)
+        w_grouped = columns[:, 0:N, :]
+        grouped = columns[:, N : N + S, :]
+        scales = keep.tile([P, N + S], U8, name="scales", align_bytes=64)
         rect = [keep.tile([P, n], F32, name=f"rect_{i}") for i, (a, n) in enumerate(PIECES)]
         y = keep.tile([P, S], F32, name="y")
         partial = keep.tile([P, V], F32, name="partial")
         result = keep.tile([P, V], F32, name="result")
         acc = [psum.tile([P, n], F32, name=f"acc_{i}") for i, (a, n) in enumerate(PIECES)]
 
-        nc.scalar.dma_start(bias[:], b)
-        nc.scalar.mul(floor[:], bias[:], -1.0)
         x_view = xT.rearrange("(p j) t -> j p t", j=4)
         for j in range(4):
             nc.sync.dma_start(raw[j][:], x_view[j])
             if j == 0:
                 nc.sync.dma_start(offsets[:], offs)
         nc.sync.dma_start(w_raw[:], w.rearrange("(p j) n -> p j n", j=4))
+        nc.sync.dma_start(bias[:], b)
         for d, pos in enumerate((pos1, pos2, pos3)):
             nc.sync.dma_start(lists[d][:], pos)
         nc.sync.dma_start(gate_first[:], gate[0])
@@ -82,30 +78,26 @@ def tile_picked_sub_lin_relu2_sub_e_kernel(tc, xT, w, b, gate, offs, pos1, pos2,
 
         def gather(j, r):
             a, n, who = RUNS[r]
-            nc.scalar.activation(rows[j // 2][r][:, j % 2, :], window(j, a, n), ACT.Copy)
+            nc.scalar.activation(rows[r][:, j - 2, :], window(j, a, n), ACT.Copy)
 
         def place(u, r):
             a, n, who = RUNS[r]
-            move(who[u], grouped[:, a : a + n, 2 * u : 2 * u + 2], rows[u][r][:].rearrange("p j n -> p n j"))
-
-        def quantize_w():
-            nc.vector.quantize_mx(
-                out=w_codes[:].bitcast(FP8X4), scales=w_scales[:], in_=w_grouped[:].rearrange("p n k -> p (n k)")
-            )
+            move(who[u], grouped[:, a : a + n, 2:4], rows[r][:].rearrange("p j n -> p n j"))
 
         def quantize(i):
             a, n = PIECES[i]
+            lo, hi = (0 if i == 0 else N + a), N + a + n
             nc.vector.quantize_mx(
-                out=codes[:, a : a + n].bitcast(FP8X4),
-                scales=scales[i][:],
-                in_=grouped[:, a : a + n, :].rearrange("p n k -> p (n k)"),
+                out=codes[:, lo:hi].bitcast(FP8X4),
+                scales=scales[:, lo:hi],
+                in_=columns[:, lo:hi, :].rearrange("p n k -> p (n k)"),
             )
             nc.tensor.matmul_mx(
                 out=acc[i][:],
-                lhsT=w_codes[:].bitcast(FP8X4),
-                lhsT_scale=w_scales[:],
-                rhs=codes[:, a : a + n].bitcast(FP8X4),
-                rhs_scale=scales[i][:],
+                lhsT=codes[:, 0:N].bitcast(FP8X4),
+                lhsT_scale=scales[:, 0:N],
+                rhs=codes[:, N + a : hi].bitcast(FP8X4),
+                rhs_scale=scales[:, N + a : hi],
                 start=True,
                 stop=True,
             )
@@ -114,7 +106,7 @@ def tile_picked_sub_lin_relu2_sub_e_kernel(tc, xT, w, b, gate, offs, pos1, pos2,
             if engine == "S":
                 nc.scalar.activation(rect[i][:, lo:hi], acc[i][:, lo:hi], ACT.Relu, bias=bias[:, 0:1])
             else:
-                nc.vector.tensor_scalar(rect[i][:, lo:hi], acc[i][:, lo:hi], floor[:, 0:1], bias[:, 0:1], ALU.max, ALU.add)
+                nc.vector.tensor_scalar(rect[i][:, lo:hi], acc[i][:, lo:hi], bias[:, 0:1], 0.0, ALU.add, ALU.max)
 
         def square(engine, i, lo, hi):
             at = PIECES[i][0]
@@ -124,21 +116,20 @@ def tile_picked_sub_lin_relu2_sub_e_kernel(tc, xT, w, b, gate, offs, pos1, pos2,
                 nc.vector.tensor_tensor(y[:, at + lo : at + hi], rect[i][:, lo:hi], rect[i][:, lo:hi], ALU.mult)
 
         w_turned = w_raw[:].rearrange("p j n -> p n j")
-        for j in range(3):
-            nc.vector.tensor_copy(grouped[:, 0:DIRECT, j], window(j, 0, DIRECT))
-            for r in range(len(RUNS)):
-                gather(j, r)
-            if j == 1:
-                for r in range(len(RUNS)):
-                    place(0, r)
+        for j in range(2):
+            nc.vector.tensor_copy(grouped[:, 0:EARLY, j], window(j, 0, EARLY))
+            nc.scalar.activation(early[:, j, :], window(j, EARLY, S - EARLY), ACT.Copy)
+        nc.vector.tensor_copy(grouped[:, EARLY:S, 0:2], early[:].rearrange("p j n -> p n j"))
+        nc.vector.tensor_copy(grouped[:, 0:DIRECT, 2], window(2, 0, DIRECT))
+        for r in range(len(RUNS)):
+            gather(2, r)
         nc.vector.tensor_copy(grouped[:, 0:DIRECT, 3], window(3, 0, DIRECT))
         for r in range(len(RUNS)):
             gather(3, r)
-        move("G", w_grouped[:], w_turned)
+        move("G", w_grouped, w_turned)
         for r in range(len(RUNS)):
             place(1, r)
-        codes = keep.tile([P, S], U32, name="codes", tag="w_raw", align_bytes=64)
-        quantize_w()
+        codes = keep.tile([P, N + S], U32, name="codes", tag="w_raw", align_bytes=64)
         for i in range(len(PIECES)):
             quantize(i)
         relu("S", 0, 0, 256)
@@ -159,23 +150,27 @@ def tile_picked_sub_lin_relu2_sub_e_kernel(tc, xT, w, b, gate, offs, pos1, pos2,
             return y[:].indirect(lists[d][:, lo // 16 : hi // 16])
 
         got_a = [keep.tile([P, 256], F32, name=f"got_a_{d}") for d in (1, 2)]
-        got_b = keep.tile([P, 256], F32, name="got_b")
+        got_b = keep.tile([P, 192], F32, name="got_b")
         first = keep.tile([P, V], F32, name="first")
         second = keep.tile([P, 256], F32, name="second")
         third = keep.tile([P, 256], F32, name="third")
         scaled = [keep.tile([P, 256], F32, name=f"scaled_{d}") for d in (1, 2)]
-        turned = [psum.tile([P, 256], F32, name=f"turned_{d}", tag=f"acc_{d - 1}") for d in (1, 2)]
-        back = [psum.tile([P, P], F32, name=f"back_{c}", tag=f"acc_{2 + c}") for c in range(2)]
-        for d in (1, 2):
-            nc.scalar.activation(got_a[d - 1][:], picked(d, 0, 256), ACT.Copy)
-            for c in range(2):
-                nc.tensor.transpose(turned[d - 1][:, c * P : (c + 1) * P], got_a[d - 1][:, c * P : (c + 1) * P], identity[:])
-        nc.scalar.activation(got_b[:], picked(2, 256, 512), ACT.Copy)
+        turned = [
+            [psum.tile([P, P], F32, name=f"turned_{d}_{c}", tag=f"acc_{2 * (d - 1) + c}") for c in range(2)] for d in (1, 2)
+        ]
+        back = [psum.tile([P, P], F32, name=f"back_{c}") for c in range(2)]
+        nc.scalar.activation(got_a[0][:], picked(1, 0, 256), ACT.Copy)
+        for c in range(2):
+            nc.tensor.transpose(turned[0][c][:], got_a[0][:, c * P : (c + 1) * P], identity[:])
+        for c in range(2):
+            nc.scalar.activation(got_a[1][:, c * P : (c + 1) * P], picked(2, c * P, (c + 1) * P), ACT.Copy)
+            nc.tensor.transpose(turned[1][c][:], got_a[1][:, c * P : (c + 1) * P], identity[:])
+        nc.scalar.activation(got_b[:], picked(2, 256, 448), ACT.Copy)
         for d in (1, 2):
             for c in range(2):
                 nc.scalar.activation(
                     scaled[d - 1][:, c * P : (c + 1) * P],
-                    turned[d - 1][:, c * P : (c + 1) * P],
+                    turned[d - 1][c][:],
                     ACT.Copy,
                     scale=gate_turned[d - 1][:, c : c + 1],
                 )
@@ -190,8 +185,9 @@ def tile_picked_sub_lin_relu2_sub_e_kernel(tc, xT, w, b, gate, offs, pos1, pos2,
         nc.vector.tensor_tensor(first[:, 256:512], picked(0, 256, 512), gate_first[:, 256:512], ALU.mult)
         nc.vector.tensor_tensor(second[:], picked(1, 256, 512), gate_rest[:, 0, :], ALU.mult)
         nc.vector.tensor_tensor(first[:, 0:256], picked(0, 0, 256), gate_first[:, 0:256], ALU.mult)
+        nc.vector.tensor_tensor(third[:, 192:256], picked(2, 448, 512), gate_rest[:, 1, 192:256], ALU.mult)
         nc.vector.tensor_tensor(partial[:, 256:512], first[:, 256:512], second[:], ALU.add)
-        nc.vector.tensor_tensor(third[:], got_b[:], gate_rest[:, 1, :], ALU.mult)
+        nc.vector.tensor_tensor(third[:, 0:192], got_b[:], gate_rest[:, 1, 0:192], ALU.mult)
         nc.vector.tensor_tensor(result[:, 0:128], first[:, 0:128], back[0][:], ALU.add)
         nc.vector.tensor_tensor(result[:, 256:512], partial[:, 256:512], third[:], ALU.add)
         store(256, 512)

@@ -18,7 +18,7 @@ ALU = mybir.AluOpType
 
 DIRECT = 448
 EARLY = 544
-RUNS = ((448, 192, "VV"), (640, 128, "VS"), (768, 256, "VS"))
+RUNS = ((448, 224, "VV"), (672, 96, "VS"), (768, 256, "VS"))
 PIECES = ((0, 256), (256, 256), (512, 256), (768, 128), (896, 128))
 
 
@@ -82,7 +82,10 @@ def tile_picked_sub_lin_relu2_sub_e_kernel(tc, xT, w, b, gate, offs, pos1, pos2,
 
         def place(u, r):
             a, n, who = RUNS[r]
-            move(who[u], grouped[:, a : a + n, 2:4], rows[r][:].rearrange("p j n -> p n j"))
+            pairs = rows[r][:].rearrange("p j n -> p n j")
+            step = n if who[u] == "V" else min(n, P)
+            for at in range(0, n, step):
+                move(who[u], grouped[:, a + at : a + at + step, 2:4], pairs[:, at : at + step, :])
 
         def quantize(i):
             a, n = PIECES[i]

@@ -16,10 +16,11 @@ FP8X4 = mybir.dt.float8_e4m3fn_x4
 ACT = mybir.ActivationFunctionType
 ALU = mybir.AluOpType
 
+LINE = 256
 DIRECT = 448
 EARLY = 544
 RUNS = ((448, 224, "VV"), (672, 96, "VS"), (768, 256, "VS"))
-PIECES = ((0, 256), (256, 256), (512, 256), (768, 128), (896, 128))
+PIECES = ((0, 256), (256, 256), (512, 256), (768, 128), (896, 64), (960, 64))
 
 
 def tile_picked_sub_lin_relu2_sub_e_kernel(tc, xT, w, b, gate, offs, pos1, pos2, pos3, out):
@@ -28,26 +29,26 @@ def tile_picked_sub_lin_relu2_sub_e_kernel(tc, xT, w, b, gate, offs, pos1, pos2,
         keep = ctx.enter_context(tc.tile_pool(name="keep", bufs=1))
         psum = ctx.enter_context(tc.psum_pool(name="psum", bufs=1))
 
-        raw = [keep.tile([P, T], F32, name=f"raw_{j}") for j in range(4)]
+        raw = [keep.tile([P, T], F32, name=f"raw_{j}", align_bytes=LINE) for j in range(4)]
         offsets = keep.tile([P, S // 16], U16, name="offsets")
         lists = [keep.tile([P, V // 16], U16, name=f"list_{d}") for d in range(D)]
-        gate_first = keep.tile([P, V], F32, name="gate_first")
-        gate_rest = keep.tile([P, 2, 256], F32, name="gate_rest")
+        gate_first = keep.tile([P, V], F32, name="gate_first", align_bytes=LINE)
+        gate_rest = keep.tile([P, 2, 256], F32, name="gate_rest", align_bytes=LINE)
         gate_turned = [keep.tile([P, 2], F32, name=f"gate_turned_{d}") for d in (1, 2)]
-        identity = keep.tile([P, P], F32, name="identity")
+        identity = keep.tile([P, P], F32, name="identity", align_bytes=LINE)
         make_identity(nc, identity[:])
-        w_raw = keep.tile([P, 4, N], F32, name="w_raw", align_bytes=64)
+        w_raw = keep.tile([P, 4, N], F32, name="w_raw", align_bytes=LINE)
         bias = keep.tile([P, 1], F32, name="bias")
-        early = keep.tile([P, 2, S - EARLY], BF16, name="early", align_bytes=64)
-        rows = [keep.tile([P, 2, n], BF16, name=f"rows_{r}", align_bytes=64) for r, (a, n, who) in enumerate(RUNS)]
-        columns = keep.tile([P, N + S, 4], BF16, name="columns", align_bytes=64)
+        early = keep.tile([P, 2, S - EARLY], BF16, name="early", align_bytes=LINE)
+        rows = [keep.tile([P, 2, n], BF16, name=f"rows_{r}", align_bytes=LINE) for r, (a, n, who) in enumerate(RUNS)]
+        columns = keep.tile([P, N + S, 4], BF16, name="columns", align_bytes=LINE)
         w_grouped = columns[:, 0:N, :]
         grouped = columns[:, N : N + S, :]
-        scales = keep.tile([P, N + S], U8, name="scales", align_bytes=64)
-        rect = [keep.tile([P, n], F32, name=f"rect_{i}") for i, (a, n) in enumerate(PIECES)]
-        y = keep.tile([P, S], F32, name="y")
-        partial = keep.tile([P, V], F32, name="partial")
-        result = keep.tile([P, V], F32, name="result")
+        scales = keep.tile([P, N + S], U8, name="scales", align_bytes=LINE)
+        rect = keep.tile([P, S], F32, name="rect", align_bytes=LINE)
+        y = keep.tile([P, S], F32, name="y", align_bytes=LINE)
+        partial = keep.tile([P, V], F32, name="partial", align_bytes=LINE)
+        result = keep.tile([P, V], F32, name="result", align_bytes=LINE)
         acc = [psum.tile([P, n], F32, name=f"acc_{i}") for i, (a, n) in enumerate(PIECES)]
 
         x_view = xT.rearrange("(p j) t -> j p t", j=4)
@@ -105,18 +106,18 @@ def tile_picked_sub_lin_relu2_sub_e_kernel(tc, xT, w, b, gate, offs, pos1, pos2,
                 stop=True,
             )
 
-        def relu(engine, i, lo, hi):
+        def relu(engine, i):
+            a, n = PIECES[i]
             if engine == "S":
-                nc.scalar.activation(rect[i][:, lo:hi], acc[i][:, lo:hi], ACT.Relu, bias=bias[:, 0:1])
+                nc.scalar.activation(rect[:, a : a + n], acc[i][:], ACT.Relu, bias=bias[:, 0:1])
             else:
-                nc.vector.tensor_scalar(rect[i][:, lo:hi], acc[i][:, lo:hi], bias[:, 0:1], 0.0, ALU.add, ALU.max)
+                nc.vector.tensor_scalar(rect[:, a : a + n], acc[i][:], bias[:, 0:1], 0.0, ALU.add, ALU.max)
 
-        def square(engine, i, lo, hi):
-            at = PIECES[i][0]
+        def square(engine, lo, hi):
             if engine == "S":
-                nc.scalar.activation(y[:, at + lo : at + hi], rect[i][:, lo:hi], ACT.Square)
+                nc.scalar.activation(y[:, lo:hi], rect[:, lo:hi], ACT.Square)
             else:
-                nc.vector.tensor_tensor(y[:, at + lo : at + hi], rect[i][:, lo:hi], rect[i][:, lo:hi], ALU.mult)
+                nc.vector.tensor_tensor(y[:, lo:hi], rect[:, lo:hi], rect[:, lo:hi], ALU.mult)
 
         w_turned = w_raw[:].rearrange("p j n -> p n j")
         for j in range(2):
@@ -132,19 +133,19 @@ def tile_picked_sub_lin_relu2_sub_e_kernel(tc, xT, w, b, gate, offs, pos1, pos2,
         move("G", w_grouped, w_turned)
         for r in range(len(RUNS)):
             place(1, r)
-        codes = keep.tile([P, N + S], U32, name="codes", tag="w_raw", align_bytes=64)
+        codes = keep.tile([P, N + S], U32, name="codes", tag="w_raw", align_bytes=LINE)
         for i in range(len(PIECES)):
             quantize(i)
-        relu("S", 0, 0, 256)
-        relu("S", 1, 0, 256)
-        square("V", 0, 0, 256)
-        relu("S", 2, 0, 256)
-        relu("V", 3, 0, 128)
-        relu("V", 4, 0, 128)
-        square("S", 1, 0, 256)
-        square("V", 2, 0, 256)
-        square("S", 3, 0, 128)
-        square("S", 4, 0, 128)
+        relu("S", 0)
+        relu("S", 1)
+        square("V", 0, 256)
+        relu("S", 2)
+        for i in (3, 4, 5):
+            relu("V", i)
+        square("S", 256, 512)
+        square("V", 512, 768)
+        square("S", 768, 960)
+        square("S", 960, 1024)
 
         def store(lo, hi):
             nc.sync.dma_start(out[:, lo:hi], result[:, lo:hi])
@@ -152,12 +153,12 @@ def tile_picked_sub_lin_relu2_sub_e_kernel(tc, xT, w, b, gate, offs, pos1, pos2,
         def picked(d, lo, hi):
             return y[:].indirect(lists[d][:, lo // 16 : hi // 16])
 
-        got_a = [keep.tile([P, 256], F32, name=f"got_a_{d}") for d in (1, 2)]
-        got_b = keep.tile([P, 192], F32, name="got_b")
-        first = keep.tile([P, V], F32, name="first")
-        second = keep.tile([P, 256], F32, name="second")
-        third = keep.tile([P, 256], F32, name="third")
-        scaled = [keep.tile([P, 256], F32, name=f"scaled_{d}") for d in (1, 2)]
+        got_a = [keep.tile([P, 256], F32, name=f"got_a_{d}", align_bytes=LINE) for d in (1, 2)]
+        got_b = keep.tile([P, 192], F32, name="got_b", align_bytes=LINE)
+        first = keep.tile([P, V], F32, name="first", align_bytes=LINE)
+        second = keep.tile([P, 256], F32, name="second", align_bytes=LINE)
+        third = keep.tile([P, 256], F32, name="third", align_bytes=LINE)
+        scaled = [keep.tile([P, 256], F32, name=f"scaled_{d}", align_bytes=LINE) for d in (1, 2)]
         turned = [
             [psum.tile([P, P], F32, name=f"turned_{d}_{c}", tag=f"acc_{2 * (d - 1) + c}") for c in range(2)] for d in (1, 2)
         ]
@@ -185,9 +186,8 @@ def tile_picked_sub_lin_relu2_sub_e_kernel(tc, xT, w, b, gate, offs, pos1, pos2,
                     stop=(d == 2),
                     is_transpose=True,
                 )
-        nc.vector.tensor_tensor(first[:, 256:512], picked(0, 256, 512), gate_first[:, 256:512], ALU.mult)
         nc.vector.tensor_tensor(second[:], picked(1, 256, 512), gate_rest[:, 0, :], ALU.mult)
-        nc.vector.tensor_tensor(first[:, 0:256], picked(0, 0, 256), gate_first[:, 0:256], ALU.mult)
+        nc.vector.tensor_tensor(first[:], picked(0, 0, V), gate_first[:], ALU.mult)
         nc.vector.tensor_tensor(third[:, 192:256], picked(2, 448, 512), gate_rest[:, 1, 192:256], ALU.mult)
         nc.vector.tensor_tensor(partial[:, 256:512], first[:, 256:512], second[:], ALU.add)
         nc.vector.tensor_tensor(third[:, 0:192], got_b[:], gate_rest[:, 1, 0:192], ALU.mult)

@@ -17,9 +17,8 @@ ACT = mybir.ActivationFunctionType
 ALU = mybir.AluOpType
 
 LINE = 256
-DIRECT = 448
-EARLY = 544
-RUNS = ((448, 224, "VV"), (672, 96, "VS"), (768, 256, "VS"))
+ON_VECTOR = (768, 512, 448, 576)
+LAID_BY_VECTOR = 512
 PIECES = ((0, 256), (256, 256), (512, 256), (768, 128), (896, 64), (960, 64))
 
 
@@ -39,8 +38,7 @@ def tile_picked_sub_lin_relu2_sub_e_kernel(tc, xT, w, b, gate, offs, pos1, pos2,
         make_identity(nc, identity[:])
         w_raw = keep.tile([P, 4, N], F32, name="w_raw", align_bytes=LINE)
         bias = keep.tile([P, 1], F32, name="bias")
-        early = keep.tile([P, 2, S - EARLY], BF16, name="early", align_bytes=LINE)
-        rows = [keep.tile([P, 2, n], BF16, name=f"rows_{r}", align_bytes=LINE) for r, (a, n, who) in enumerate(RUNS)]
+        rows = [keep.tile([P, 2, S], BF16, name=f"rows_{u}", align_bytes=LINE) for u in range(2)]
         columns = keep.tile([P, N + S, 4], BF16, name="columns", align_bytes=LINE)
         w_grouped = columns[:, 0:N, :]
         grouped = columns[:, N : N + S, :]
@@ -66,27 +64,23 @@ def tile_picked_sub_lin_relu2_sub_e_kernel(tc, xT, w, b, gate, offs, pos1, pos2,
             for d in (1, 2):
                 nc.sync.dma_start(gate_turned[d - 1][:], gate[d, 0, 0:256].rearrange("(c p) -> p c", p=P))
 
-        def window(j, a, n):
-            return raw[j][:].indirect(offsets[:, a // 16 : (a + n) // 16])
+        def window(j, lo, hi):
+            return raw[j][:].indirect(offsets[:, lo // 16 : hi // 16])
 
-        def move(who, dst, src):
-            if who == "S":
+        def gather(engine, j, lo, hi):
+            row = rows[j // 2][:, j % 2, lo:hi]
+            if engine == "S":
+                nc.scalar.activation(row, window(j, lo, hi), ACT.Copy)
+            else:
+                nc.vector.tensor_copy(row, window(j, lo, hi))
+
+        def lay(engine, u, lo, hi):
+            dst = grouped[:, lo:hi, 2 * u : 2 * u + 2]
+            src = rows[u][:, :, lo:hi].rearrange("p j n -> p n j")
+            if engine == "S":
                 nc.scalar.copy(dst, src)
-            elif who == "G":
-                nc.gpsimd.tensor_scalar(dst, src, 1.0, 0.0, ALU.mult, ALU.add)
             else:
                 nc.vector.tensor_copy(dst, src)
-
-        def gather(j, r):
-            a, n, who = RUNS[r]
-            nc.scalar.activation(rows[r][:, j - 2, :], window(j, a, n), ACT.Copy)
-
-        def place(u, r):
-            a, n, who = RUNS[r]
-            pairs = rows[r][:].rearrange("p j n -> p n j")
-            step = n if who[u] == "V" else min(n, P)
-            for at in range(0, n, step):
-                move(who[u], grouped[:, a + at : a + at + step, 2:4], pairs[:, at : at + step, :])
 
         def quantize(i):
             a, n = PIECES[i]
@@ -119,22 +113,25 @@ def tile_picked_sub_lin_relu2_sub_e_kernel(tc, xT, w, b, gate, offs, pos1, pos2,
             else:
                 nc.vector.tensor_tensor(y[:, lo:hi], rect[:, lo:hi], rect[:, lo:hi], ALU.mult)
 
-        w_turned = w_raw[:].rearrange("p j n -> p n j")
         for j in range(2):
-            nc.vector.tensor_copy(grouped[:, 0:EARLY, j], window(j, 0, EARLY))
-            nc.scalar.activation(early[:, j, :], window(j, EARLY, S - EARLY), ACT.Copy)
-        nc.vector.tensor_copy(grouped[:, EARLY:S, 0:2], early[:].rearrange("p j n -> p n j"))
-        nc.vector.tensor_copy(grouped[:, 0:DIRECT, 2], window(2, 0, DIRECT))
-        for r in range(len(RUNS)):
-            gather(2, r)
-        nc.vector.tensor_copy(grouped[:, 0:DIRECT, 3], window(3, 0, DIRECT))
-        for r in range(len(RUNS)):
-            gather(3, r)
-        move("G", w_grouped, w_turned)
-        for r in range(len(RUNS)):
-            place(1, r)
+            gather("V", j, 0, ON_VECTOR[j])
+            gather("S", j, ON_VECTOR[j], S)
+        lay("V", 0, 0, ON_VECTOR[1])
+        gather("V", 2, 0, ON_VECTOR[2])
+        gather("S", 2, ON_VECTOR[2], S)
+        lay("V", 0, ON_VECTOR[1], S)
+        gather("V", 3, 0, 256)
+        gather("V", 3, 256, ON_VECTOR[3])
+        gather("S", 3, 768, S)
+        gather("S", 3, ON_VECTOR[3], 768)
+        nc.gpsimd.tensor_scalar(w_grouped, w_raw[:].rearrange("p j n -> p n j"), 1.0, 0.0, ALU.mult, ALU.add)
+        lay("V", 1, 0, 256)
+        lay("V", 1, 256, LAID_BY_VECTOR)
+        lay("S", 1, 768, 896)
+        lay("S", 1, LAID_BY_VECTOR, 768)
+        lay("S", 1, 896, S)
         codes = keep.tile([P, N + S], U32, name="codes", tag="w_raw", align_bytes=LINE)
-        for i in range(len(PIECES)):
+        for i in (0, 1, 3, 2, 4, 5):
             quantize(i)
         relu("S", 0)
         relu("S", 1)

@@ -17,8 +17,11 @@ ACT = mybir.ActivationFunctionType
 ALU = mybir.AluOpType
 
 LINE = 256
-ON_VECTOR = (768, 512, 448, 576)
-LAID_BY_VECTOR = 512
+DIRECT = 320
+ON_VECTOR = (480, 480, 480, 416)
+LAID_BY_VECTOR = 704
+RUN_CUT = 768
+ROW = (1, 2, 0, 1)
 PIECES = ((0, 256), (256, 256), (512, 256), (768, 128), (896, 64), (960, 64))
 
 
@@ -36,9 +39,13 @@ def tile_picked_sub_lin_relu2_sub_e_kernel(tc, xT, w, b, gate, offs, pos1, pos2,
         gate_turned = [keep.tile([P, 2], F32, name=f"gate_turned_{d}") for d in (1, 2)]
         identity = keep.tile([P, P], F32, name="identity", align_bytes=LINE)
         make_identity(nc, identity[:])
+        unread = keep.tile([P, 1], F32, name="unread")
+        zero = keep.tile([P, 1], F32, name="zero")
+        nc.vector.memset(zero[:], 0.0)
+        nc.scalar.activation(unread[:], zero[:], ACT.Copy)
         w_raw = keep.tile([P, 4, N], F32, name="w_raw", align_bytes=LINE)
         bias = keep.tile([P, 1], F32, name="bias")
-        rows = [keep.tile([P, 2, S], BF16, name=f"rows_{u}", align_bytes=LINE) for u in range(2)]
+        rows = keep.tile([P, 3, S], BF16, name="rows", align_bytes=LINE)
         columns = keep.tile([P, N + S, 4], BF16, name="columns", align_bytes=LINE)
         w_grouped = columns[:, 0:N, :]
         grouped = columns[:, N : N + S, :]
@@ -67,18 +74,25 @@ def tile_picked_sub_lin_relu2_sub_e_kernel(tc, xT, w, b, gate, offs, pos1, pos2,
         def window(j, lo, hi):
             return raw[j][:].indirect(offsets[:, lo // 16 : hi // 16])
 
+        def direct(j):
+            nc.vector.tensor_copy(grouped[:, 0:DIRECT, j], window(j, 0, DIRECT))
+
         def gather(engine, j, lo, hi):
-            row = rows[j // 2][:, j % 2, lo:hi]
             if engine == "S":
-                nc.scalar.activation(row, window(j, lo, hi), ACT.Copy)
+                nc.scalar.activation(rows[:, ROW[j], lo:hi], window(j, lo, hi), ACT.Copy)
             else:
-                nc.vector.tensor_copy(row, window(j, lo, hi))
+                nc.vector.tensor_copy(rows[:, ROW[j], lo:hi], window(j, lo, hi))
+
+        def on_gpsimd(dst, src):
+            nc.gpsimd.tensor_scalar(dst, src, 1.0, 0.0, ALU.mult, ALU.add)
 
         def lay(engine, u, lo, hi):
             dst = grouped[:, lo:hi, 2 * u : 2 * u + 2]
-            src = rows[u][:, :, lo:hi].rearrange("p j n -> p n j")
+            src = rows[:, ROW[2 * u] : ROW[2 * u] + 2, lo:hi].rearrange("p j n -> p n j")
             if engine == "S":
                 nc.scalar.copy(dst, src)
+            elif engine == "G":
+                on_gpsimd(dst, src)
             else:
                 nc.vector.tensor_copy(dst, src)
 
@@ -113,25 +127,29 @@ def tile_picked_sub_lin_relu2_sub_e_kernel(tc, xT, w, b, gate, offs, pos1, pos2,
             else:
                 nc.vector.tensor_tensor(y[:, lo:hi], rect[:, lo:hi], rect[:, lo:hi], ALU.mult)
 
-        for j in range(2):
-            gather("V", j, 0, ON_VECTOR[j])
-            gather("S", j, ON_VECTOR[j], S)
-        lay("V", 0, 0, ON_VECTOR[1])
-        gather("V", 2, 0, ON_VECTOR[2])
-        gather("S", 2, ON_VECTOR[2], S)
-        lay("V", 0, ON_VECTOR[1], S)
-        gather("V", 3, 0, 256)
-        gather("V", 3, 256, ON_VECTOR[3])
+        for j in range(3):
+            gather("V", j, DIRECT, ON_VECTOR[j])
+            direct(j)
+            if j == 1:
+                gather("S", j, ON_VECTOR[j], RUN_CUT)
+                gather("S", j, RUN_CUT, S)
+                lay("G", 0, DIRECT, RUN_CUT)
+                lay("G", 0, RUN_CUT, S)
+            else:
+                gather("S", j, ON_VECTOR[j], S)
+        gather("V", 3, DIRECT, ON_VECTOR[3])
+        direct(3)
+        gather("S", 3, ON_VECTOR[3], LAID_BY_VECTOR)
+        gather("S", 3, LAID_BY_VECTOR, 768)
         gather("S", 3, 768, S)
-        gather("S", 3, ON_VECTOR[3], 768)
-        nc.gpsimd.tensor_scalar(w_grouped, w_raw[:].rearrange("p j n -> p n j"), 1.0, 0.0, ALU.mult, ALU.add)
-        lay("V", 1, 0, 256)
-        lay("V", 1, 256, LAID_BY_VECTOR)
-        lay("S", 1, 768, 896)
+        on_gpsimd(w_grouped, w_raw[:].rearrange("p j n -> p n j"))
+        lay("V", 1, DIRECT, 512)
+        lay("V", 1, 512, LAID_BY_VECTOR)
         lay("S", 1, LAID_BY_VECTOR, 768)
+        lay("S", 1, 768, 896)
         lay("S", 1, 896, S)
         codes = keep.tile([P, N + S], U32, name="codes", tag="w_raw", align_bytes=LINE)
-        for i in (0, 1, 3, 2, 4, 5):
+        for i in range(len(PIECES)):
             quantize(i)
         relu("S", 0)
         relu("S", 1)

@@ -17,10 +17,10 @@ ACT = mybir.ActivationFunctionType
 ALU = mybir.AluOpType
 
 LINE = 256
-DIRECT = 320
-ON_VECTOR = (480, 480, 480, 416)
-LAID_BY_VECTOR = 704
-RUN_CUT = 768
+DIRECT = 448
+ON_VECTOR = (608, 608, 576)
+LAID_BY_VECTOR = 672
+RUN_CUT = 832
 ROW = (1, 2, 0, 1)
 PIECES = ((0, 256), (256, 256), (512, 256), (768, 128), (896, 64), (960, 64))
 
@@ -39,10 +39,6 @@ def tile_picked_sub_lin_relu2_sub_e_kernel(tc, xT, w, b, gate, offs, pos1, pos2,
         gate_turned = [keep.tile([P, 2], F32, name=f"gate_turned_{d}") for d in (1, 2)]
         identity = keep.tile([P, P], F32, name="identity", align_bytes=LINE)
         make_identity(nc, identity[:])
-        unread = keep.tile([P, 1], F32, name="unread")
-        zero = keep.tile([P, 1], F32, name="zero")
-        nc.vector.memset(zero[:], 0.0)
-        nc.scalar.activation(unread[:], zero[:], ACT.Copy)
         w_raw = keep.tile([P, 4, N], F32, name="w_raw", align_bytes=LINE)
         bias = keep.tile([P, 1], F32, name="bias")
         rows = keep.tile([P, 3, S], BF16, name="rows", align_bytes=LINE)
@@ -137,14 +133,12 @@ def tile_picked_sub_lin_relu2_sub_e_kernel(tc, xT, w, b, gate, offs, pos1, pos2,
                 lay("G", 0, RUN_CUT, S)
             else:
                 gather("S", j, ON_VECTOR[j], S)
-        gather("V", 3, DIRECT, ON_VECTOR[3])
         direct(3)
-        gather("S", 3, ON_VECTOR[3], LAID_BY_VECTOR)
+        gather("S", 3, DIRECT, LAID_BY_VECTOR)
         gather("S", 3, LAID_BY_VECTOR, 768)
         gather("S", 3, 768, S)
         on_gpsimd(w_grouped, w_raw[:].rearrange("p j n -> p n j"))
-        lay("V", 1, DIRECT, 512)
-        lay("V", 1, 512, LAID_BY_VECTOR)
+        lay("V", 1, DIRECT, LAID_BY_VECTOR)
         lay("S", 1, LAID_BY_VECTOR, 768)
         lay("S", 1, 768, 896)
         lay("S", 1, 896, S)

@@ -17,12 +17,12 @@ ACT = mybir.ActivationFunctionType
 ALU = mybir.AluOpType
 
 LINE = 256
-DIRECT = 448
+DIRECT = (448, 448, 352, 352)
 ON_VECTOR = (608, 608, 576)
-LAID_BY_VECTOR = 672
 RUN_CUT = 832
+RUNS = ((352, 544, "V"), (544, 736, "V"), (736, 896, "S"), (896, S, "S"))
 ROW = (1, 2, 0, 1)
-PIECES = ((0, 256), (256, 256), (512, 256), (768, 128), (896, 64), (960, 64))
+PIECES = ((0, 128), (128, 256), (384, 256), (640, 128), (768, 128), (896, 128))
 
 
 def tile_picked_sub_lin_relu2_sub_e_kernel(tc, xT, w, b, gate, offs, pos1, pos2, pos3, out):
@@ -70,8 +70,8 @@ def tile_picked_sub_lin_relu2_sub_e_kernel(tc, xT, w, b, gate, offs, pos1, pos2,
         def window(j, lo, hi):
             return raw[j][:].indirect(offsets[:, lo // 16 : hi // 16])
 
-        def direct(j):
-            nc.vector.tensor_copy(grouped[:, 0:DIRECT, j], window(j, 0, DIRECT))
+        def direct(j, hi):
+            nc.vector.tensor_copy(grouped[:, 0:hi, j], window(j, 0, hi))
 
         def gather(engine, j, lo, hi):
             if engine == "S":
@@ -124,37 +124,36 @@ def tile_picked_sub_lin_relu2_sub_e_kernel(tc, xT, w, b, gate, offs, pos1, pos2,
                 nc.vector.tensor_tensor(y[:, lo:hi], rect[:, lo:hi], rect[:, lo:hi], ALU.mult)
 
         for j in range(3):
-            gather("V", j, DIRECT, ON_VECTOR[j])
-            direct(j)
+            gather("V", j, DIRECT[j], ON_VECTOR[j])
+            direct(j, DIRECT[j])
             if j == 1:
                 gather("S", j, ON_VECTOR[j], RUN_CUT)
                 gather("S", j, RUN_CUT, S)
-                lay("G", 0, DIRECT, RUN_CUT)
+                lay("G", 0, DIRECT[j], RUN_CUT)
                 lay("G", 0, RUN_CUT, S)
             else:
                 gather("S", j, ON_VECTOR[j], S)
-        direct(3)
-        gather("S", 3, DIRECT, LAID_BY_VECTOR)
-        gather("S", 3, LAID_BY_VECTOR, 768)
-        gather("S", 3, 768, S)
+        direct(3, DIRECT[3])
+        for lo, hi, engine in RUNS:
+            gather("S", 3, lo, hi)
         on_gpsimd(w_grouped, w_raw[:].rearrange("p j n -> p n j"))
-        lay("V", 1, DIRECT, LAID_BY_VECTOR)
-        lay("S", 1, LAID_BY_VECTOR, 768)
-        lay("S", 1, 768, 896)
-        lay("S", 1, 896, S)
+        for lo, hi, engine in RUNS:
+            lay(engine, 1, lo, hi)
         codes = keep.tile([P, N + S], U32, name="codes", tag="w_raw", align_bytes=LINE)
         for i in range(len(PIECES)):
             quantize(i)
         relu("S", 0)
-        relu("S", 1)
-        square("V", 0, 256)
+        square("S", 0, 128)
+        relu("V", 1)
         relu("S", 2)
+        square("S", 128, 384)
         for i in (3, 4, 5):
             relu("V", i)
-        square("S", 256, 512)
-        square("V", 512, 768)
-        square("S", 768, 960)
-        square("S", 960, 1024)
+        square("V", 384, 640)
+        square("S", 640, 768)
+        square("S", 768, 896)
+        square("S", 896, 960)
+        square("V", 960, 1024)
 
         def store(lo, hi):
             nc.sync.dma_start(out[:, lo:hi], result[:, lo:hi])
@@ -178,7 +177,7 @@ def tile_picked_sub_lin_relu2_sub_e_kernel(tc, xT, w, b, gate, offs, pos1, pos2,
         for c in range(2):
             nc.scalar.activation(got_a[1][:, c * P : (c + 1) * P], picked(2, c * P, (c + 1) * P), ACT.Copy)
             nc.tensor.transpose(turned[1][c][:], got_a[1][:, c * P : (c + 1) * P], identity[:])
-        nc.scalar.activation(got_b[:], picked(2, 256, 448), ACT.Copy)
+        nc.scalar.activation(got_b[:], picked(0, 0, 192), ACT.Copy)
         for d in (1, 2):
             for c in range(2):
                 nc.scalar.activation(
@@ -196,12 +195,12 @@ def tile_picked_sub_lin_relu2_sub_e_kernel(tc, xT, w, b, gate, offs, pos1, pos2,
                     is_transpose=True,
                 )
         nc.vector.tensor_tensor(second[:], picked(1, 256, 512), gate_rest[:, 0, :], ALU.mult)
-        nc.vector.tensor_tensor(first[:], picked(0, 0, V), gate_first[:], ALU.mult)
-        nc.vector.tensor_tensor(third[:, 192:256], picked(2, 448, 512), gate_rest[:, 1, 192:256], ALU.mult)
+        nc.vector.tensor_tensor(first[:, 192:V], picked(0, 192, V), gate_first[:, 192:V], ALU.mult)
+        nc.vector.tensor_tensor(third[:], picked(2, 256, 512), gate_rest[:, 1, :], ALU.mult)
         nc.vector.tensor_tensor(partial[:, 256:512], first[:, 256:512], second[:], ALU.add)
-        nc.vector.tensor_tensor(third[:, 0:192], got_b[:], gate_rest[:, 1, 0:192], ALU.mult)
-        nc.vector.tensor_tensor(result[:, 0:128], first[:, 0:128], back[0][:], ALU.add)
+        nc.vector.tensor_tensor(first[:, 0:192], got_b[:], gate_first[:, 0:192], ALU.mult)
         nc.vector.tensor_tensor(result[:, 256:512], partial[:, 256:512], third[:], ALU.add)
         store(256, 512)
+        nc.vector.tensor_tensor(result[:, 0:128], first[:, 0:128], back[0][:], ALU.add)
         nc.vector.tensor_tensor(result[:, 128:256], first[:, 128:256], back[1][:], ALU.add)
         store(0, 256)

@@ -17,10 +17,10 @@ ACT = mybir.ActivationFunctionType
 ALU = mybir.AluOpType
 
 LINE = 256
-DIRECT = (448, 448, 352, 352)
-ON_VECTOR = (608, 608, 576)
+EARLY_DIRECT = 448
+LATE_DIRECT = 576
+ON_VECTOR = 608
 RUN_CUT = 832
-RUNS = ((352, 544, "V"), (544, 736, "V"), (736, 896, "S"), (896, S, "S"))
 ROW = (1, 2, 0, 1)
 PIECES = ((0, 128), (128, 256), (384, 256), (640, 128), (768, 128), (896, 128))
 
@@ -70,8 +70,8 @@ def tile_picked_sub_lin_relu2_sub_e_kernel(tc, xT, w, b, gate, offs, pos1, pos2,
         def window(j, lo, hi):
             return raw[j][:].indirect(offsets[:, lo // 16 : hi // 16])
 
-        def direct(j, hi):
-            nc.vector.tensor_copy(grouped[:, 0:hi, j], window(j, 0, hi))
+        def direct(j, lo, hi):
+            nc.vector.tensor_copy(grouped[:, lo:hi, j], window(j, lo, hi))
 
         def gather(engine, j, lo, hi):
             if engine == "S":
@@ -87,10 +87,8 @@ def tile_picked_sub_lin_relu2_sub_e_kernel(tc, xT, w, b, gate, offs, pos1, pos2,
             src = rows[:, ROW[2 * u] : ROW[2 * u] + 2, lo:hi].rearrange("p j n -> p n j")
             if engine == "S":
                 nc.scalar.copy(dst, src)
-            elif engine == "G":
-                on_gpsimd(dst, src)
             else:
-                nc.vector.tensor_copy(dst, src)
+                on_gpsimd(dst, src)
 
         def quantize(i):
             a, n = PIECES[i]
@@ -123,22 +121,25 @@ def tile_picked_sub_lin_relu2_sub_e_kernel(tc, xT, w, b, gate, offs, pos1, pos2,
             else:
                 nc.vector.tensor_tensor(y[:, lo:hi], rect[:, lo:hi], rect[:, lo:hi], ALU.mult)
 
-        for j in range(3):
-            gather("V", j, DIRECT[j], ON_VECTOR[j])
-            direct(j, DIRECT[j])
-            if j == 1:
-                gather("S", j, ON_VECTOR[j], RUN_CUT)
-                gather("S", j, RUN_CUT, S)
-                lay("G", 0, DIRECT[j], RUN_CUT)
-                lay("G", 0, RUN_CUT, S)
-            else:
-                gather("S", j, ON_VECTOR[j], S)
-        direct(3, DIRECT[3])
-        for lo, hi, engine in RUNS:
-            gather("S", 3, lo, hi)
+        for j in range(2):
+            gather("V", j, EARLY_DIRECT, ON_VECTOR)
+            direct(j, 0, EARLY_DIRECT)
+        gather("S", 0, ON_VECTOR, S)
+        gather("S", 1, ON_VECTOR, RUN_CUT)
+        gather("S", 1, RUN_CUT, S)
+        lay("S", 0, EARLY_DIRECT, LATE_DIRECT)
+        lay("G", 0, LATE_DIRECT, RUN_CUT)
+        lay("G", 0, RUN_CUT, S)
+        direct(2, 0, LATE_DIRECT)
+        gather("S", 2, LATE_DIRECT, S)
+        direct(3, 0, LATE_DIRECT // 2)
+        direct(3, LATE_DIRECT // 2, LATE_DIRECT)
+        gather("S", 3, LATE_DIRECT, 768)
+        gather("S", 3, 768, S)
         on_gpsimd(w_grouped, w_raw[:].rearrange("p j n -> p n j"))
-        for lo, hi, engine in RUNS:
-            lay(engine, 1, lo, hi)
+        lay("S", 1, LATE_DIRECT, 768)
+        lay("S", 1, 768, 896)
+        lay("S", 1, 896, S)
         codes = keep.tile([P, N + S], U32, name="codes", tag="w_raw", align_bytes=LINE)
         for i in range(len(PIECES)):
             quantize(i)
@@ -162,7 +163,7 @@ def tile_picked_sub_lin_relu2_sub_e_kernel(tc, xT, w, b, gate, offs, pos1, pos2,
             return y[:].indirect(lists[d][:, lo // 16 : hi // 16])
 
         got_a = [keep.tile([P, 256], F32, name=f"got_a_{d}", align_bytes=LINE) for d in (1, 2)]
-        got_b = keep.tile([P, 192], F32, name="got_b", align_bytes=LINE)
+        got_b = keep.tile([P, P], F32, name="got_b", align_bytes=LINE)
         first = keep.tile([P, V], F32, name="first", align_bytes=LINE)
         second = keep.tile([P, 256], F32, name="second", align_bytes=LINE)
         third = keep.tile([P, 256], F32, name="third", align_bytes=LINE)
@@ -177,7 +178,7 @@ def tile_picked_sub_lin_relu2_sub_e_kernel(tc, xT, w, b, gate, offs, pos1, pos2,
         for c in range(2):
             nc.scalar.activation(got_a[1][:, c * P : (c + 1) * P], picked(2, c * P, (c + 1) * P), ACT.Copy)
             nc.tensor.transpose(turned[1][c][:], got_a[1][:, c * P : (c + 1) * P], identity[:])
-        nc.scalar.activation(got_b[:], picked(0, 0, 192), ACT.Copy)
+        nc.scalar.activation(got_b[:], picked(0, P, 256), ACT.Copy)
         for d in (1, 2):
             for c in range(2):
                 nc.scalar.activation(
@@ -195,12 +196,14 @@ def tile_picked_sub_lin_relu2_sub_e_kernel(tc, xT, w, b, gate, offs, pos1, pos2,
                     is_transpose=True,
                 )
         nc.vector.tensor_tensor(second[:], picked(1, 256, 512), gate_rest[:, 0, :], ALU.mult)
-        nc.vector.tensor_tensor(first[:, 192:V], picked(0, 192, V), gate_first[:, 192:V], ALU.mult)
+        nc.vector.tensor_tensor(first[:, 256:V], picked(0, 256, V), gate_first[:, 256:V], ALU.mult)
         nc.vector.tensor_tensor(third[:], picked(2, 256, 512), gate_rest[:, 1, :], ALU.mult)
         nc.vector.tensor_tensor(partial[:, 256:512], first[:, 256:512], second[:], ALU.add)
-        nc.vector.tensor_tensor(first[:, 0:192], got_b[:], gate_first[:, 0:192], ALU.mult)
+        first_quarter = gate_rest[:, 1, 0:P]
+        nc.vector.tensor_tensor(first_quarter, picked(0, 0, P), gate_first[:, 0:P], ALU.mult)
         nc.vector.tensor_tensor(result[:, 256:512], partial[:, 256:512], third[:], ALU.add)
         store(256, 512)
-        nc.vector.tensor_tensor(result[:, 0:128], first[:, 0:128], back[0][:], ALU.add)
+        nc.vector.tensor_tensor(first[:, P:256], got_b[:], gate_first[:, P:256], ALU.mult)
+        nc.vector.tensor_tensor(result[:, 0:128], first_quarter, back[0][:], ALU.add)
         nc.vector.tensor_tensor(result[:, 128:256], first[:, 128:256], back[1][:], ALU.add)
         store(0, 256)

from contextlib import ExitStack

import concourse.mybir as mybir
from concourse.masks import make_identity

K, T, D, S, V, N = 512, 2048, 3, 1024, 512, 128
P = 128
FLOPS = 2 * K * N * S

F32 = mybir.dt.float32
BF16 = mybir.dt.bfloat16
U32 = mybir.dt.uint32
U16 = mybir.dt.uint16
U8 = mybir.dt.uint8
FP8X4 = mybir.dt.float8_e4m3fn_x4
ACT = mybir.ActivationFunctionType
ALU = mybir.AluOpType

LINE = 256
EARLY_DIRECT = 448
LATE_DIRECT = 576
ON_VECTOR = 608
RUN_CUT = 832
ROW = (1, 2, 0, 1)
PIECES = ((0, 128), (128, 256), (384, 256), (640, 128), (768, 128), (896, 128))


def tile_picked_sub_lin_relu2_sub_e_kernel(tc, xT, w, b, gate, offs, pos1, pos2, pos3, out):
    nc = tc.nc
    with ExitStack() as ctx:
        keep = ctx.enter_context(tc.tile_pool(name="keep", bufs=1))
        psum = ctx.enter_context(tc.psum_pool(name="psum", bufs=1))

        raw = [keep.tile([P, T], F32, name=f"raw_{j}", align_bytes=LINE) for j in range(4)]
        offsets = keep.tile([P, S // 16], U16, name="offsets")
        lists = [keep.tile([P, V // 16], U16, name=f"list_{d}") for d in range(D)]
        gate_first = keep.tile([P, V], F32, name="gate_first", align_bytes=LINE)
        gate_rest = keep.tile([P, 2, 256], F32, name="gate_rest", align_bytes=LINE)
        gate_turned = [keep.tile([P, 2], F32, name=f"gate_turned_{d}") for d in (1, 2)]
        identity = keep.tile([P, P], F32, name="identity", align_bytes=LINE)
        make_identity(nc, identity[:])
        w_raw = keep.tile([P, 4, N], F32, name="w_raw", align_bytes=LINE)
        bias = keep.tile([P, 1], F32, name="bias")
        rows = keep.tile([P, 3, S], BF16, name="rows", align_bytes=LINE)
        columns = keep.tile([P, N + S, 4], BF16, name="columns", align_bytes=LINE)
        w_grouped = columns[:, 0:N, :]
        grouped = columns[:, N : N + S, :]
        scales = keep.tile([P, N + S], U8, name="scales", align_bytes=LINE)
        rect = keep.tile([P, S], F32, name="rect", align_bytes=LINE)
        y = keep.tile([P, S], F32, name="y", align_bytes=LINE)
        partial = keep.tile([P, V], F32, name="partial", align_bytes=LINE)
        result = keep.tile([P, V], F32, name="result", align_bytes=LINE)
        acc = [psum.tile([P, n], F32, name=f"acc_{i}") for i, (a, n) in enumerate(PIECES)]

        x_view = xT.rearrange("(p j) t -> j p t", j=4)
        for j in range(4):
            nc.sync.dma_start(raw[j][:], x_view[j])
            if j == 0:
                nc.sync.dma_start(offsets[:], offs)
        nc.sync.dma_start(w_raw[:], w.rearrange("(p j) n -> p j n", j=4))
        nc.sync.dma_start(bias[:], b)
        for d, pos in enumerate((pos1, pos2, pos3)):
            nc.sync.dma_start(lists[d][:], pos)
        nc.sync.dma_start(gate_first[:], gate[0])
        nc.sync.dma_start(gate_rest[:], gate[1:3, :, 256:512].rearrange("d p v -> p d v"))
        with nc.allow_non_contiguous_dma(reason="one gate value a partition"):
            for d in (1, 2):
                nc.sync.dma_start(gate_turned[d - 1][:], gate[d, 0, 0:256].rearrange("(c p) -> p c", p=P))

        def window(j, lo, hi):
            return raw[j][:].indirect(offsets[:, lo // 16 : hi // 16])

        def direct(j, lo, hi):
            nc.vector.tensor_copy(grouped[:, lo:hi, j], window(j, lo, hi))

        def gather(engine, j, lo, hi):
            if engine == "S":
                nc.scalar.activation(rows[:, ROW[j], lo:hi], window(j, lo, hi), ACT.Copy)
            else:
                nc.vector.tensor_copy(rows[:, ROW[j], lo:hi], window(j, lo, hi))

        def on_gpsimd(dst, src):
            nc.gpsimd.tensor_scalar(dst, src, 1.0, 0.0, ALU.mult, ALU.add)

        def lay(engine, u, lo, hi):
            dst = grouped[:, lo:hi, 2 * u : 2 * u + 2]
            src = rows[:, ROW[2 * u] : ROW[2 * u] + 2, lo:hi].rearrange("p j n -> p n j")
            if engine == "S":
                nc.scalar.copy(dst, src)
            else:
                on_gpsimd(dst, src)

        def quantize(i):
            a, n = PIECES[i]
            lo, hi = (0 if i == 0 else N + a), N + a + n
            nc.vector.quantize_mx(
                out=codes[:, lo:hi].bitcast(FP8X4),
                scales=scales[:, lo:hi],
                in_=columns[:, lo:hi, :].rearrange("p n k -> p (n k)"),
            )
            nc.tensor.matmul_mx(
                out=acc[i][:],
                lhsT=codes[:, 0:N].bitcast(FP8X4),
                lhsT_scale=scales[:, 0:N],
                rhs=codes[:, N + a : hi].bitcast(FP8X4),
                rhs_scale=scales[:, N + a : hi],
                start=True,
                stop=True,
            )

        def relu(engine, i):
            a, n = PIECES[i]
            if engine == "S":
                nc.scalar.activation(rect[:, a : a + n], acc[i][:], ACT.Relu, bias=bias[:, 0:1])
            else:
                nc.vector.tensor_scalar(rect[:, a : a + n], acc[i][:], bias[:, 0:1], 0.0, ALU.add, ALU.max)

        def square(engine, lo, hi):
            if engine == "S":
                nc.scalar.activation(y[:, lo:hi], rect[:, lo:hi], ACT.Square)
            else:
                nc.vector.tensor_tensor(y[:, lo:hi], rect[:, lo:hi], rect[:, lo:hi], ALU.mult)

        for j in range(2):
            gather("V", j, EARLY_DIRECT, ON_VECTOR)
            direct(j, 0, EARLY_DIRECT)
        gather("S", 0, ON_VECTOR, S)
        gather("S", 1, ON_VECTOR, RUN_CUT)
        gather("S", 1, RUN_CUT, S)
        lay("S", 0, EARLY_DIRECT, LATE_DIRECT)
        lay("G", 0, LATE_DIRECT, RUN_CUT)
        lay("G", 0, RUN_CUT, S)
        direct(2, 0, LATE_DIRECT)
        gather("S", 2, LATE_DIRECT, S)
        direct(3, 0, LATE_DIRECT // 2)
        direct(3, LATE_DIRECT // 2, LATE_DIRECT)
        gather("S", 3, LATE_DIRECT, 768)
        gather("S", 3, 768, S)
        on_gpsimd(w_grouped, w_raw[:].rearrange("p j n -> p n j"))
        lay("S", 1, LATE_DIRECT, 768)
        lay("S", 1, 768, 896)
        lay("S", 1, 896, S)
        codes = keep.tile([P, N + S], U32, name="codes", tag="w_raw", align_bytes=LINE)
        for i in range(len(PIECES)):
            quantize(i)
        relu("S", 0)
        square("S", 0, 128)
        relu("V", 1)
        relu("S", 2)
        square("S", 128, 384)
        for i in (3, 4, 5):
            relu("V", i)
        square("V", 384, 640)
        square("S", 640, 768)
        square("S", 768, 896)
        square("S", 896, 960)
        square("V", 960, 1024)

        def store(lo, hi):
            nc.sync.dma_start(out[:, lo:hi], result[:, lo:hi])

        def picked(d, lo, hi):
            return y[:].indirect(lists[d][:, lo // 16 : hi // 16])

        got_a = [keep.tile([P, 256], F32, name=f"got_a_{d}", align_bytes=LINE) for d in (1, 2)]
        got_b = keep.tile([P, P], F32, name="got_b", align_bytes=LINE)
        first = keep.tile([P, V], F32, name="first", align_bytes=LINE)
        second = keep.tile([P, 256], F32, name="second", align_bytes=LINE)
        third = keep.tile([P, 256], F32, name="third", align_bytes=LINE)
        scaled = [keep.tile([P, 256], F32, name=f"scaled_{d}", align_bytes=LINE) for d in (1, 2)]
        turned = [
            [psum.tile([P, P], F32, name=f"turned_{d}_{c}", tag=f"acc_{2 * (d - 1) + c}") for c in range(2)] for d in (1, 2)
        ]
        back = [psum.tile([P, P], F32, name=f"back_{c}") for c in range(2)]
        nc.scalar.activation(got_a[0][:], picked(1, 0, 256), ACT.Copy)
        for c in range(2):
            nc.tensor.transpose(turned[0][c][:], got_a[0][:, c * P : (c + 1) * P], identity[:])
        for c in range(2):
            nc.scalar.activation(got_a[1][:, c * P : (c + 1) * P], picked(2, c * P, (c + 1) * P), ACT.Copy)
            nc.tensor.transpose(turned[1][c][:], got_a[1][:, c * P : (c + 1) * P], identity[:])
        nc.scalar.activation(got_b[:], picked(0, P, 256), ACT.Copy)
        for d in (1, 2):
            for c in range(2):
                nc.scalar.activation(
                    scaled[d - 1][:, c * P : (c + 1) * P],
                    turned[d - 1][c][:],
                    ACT.Copy,
                    scale=gate_turned[d - 1][:, c : c + 1],
                )
                nc.tensor.matmul(
                    back[c][:],
                    lhsT=scaled[d - 1][:, c * P : (c + 1) * P],
                    rhs=identity[:],
                    start=(d == 1),
                    stop=(d == 2),
                    is_transpose=True,
                )
        nc.vector.tensor_tensor(second[:], picked(1, 256, 512), gate_rest[:, 0, :], ALU.mult)
        nc.vector.tensor_tensor(first[:, 256:V], picked(0, 256, V), gate_first[:, 256:V], ALU.mult)
        nc.vector.tensor_tensor(third[:], picked(2, 256, 512), gate_rest[:, 1, :], ALU.mult)
        nc.vector.tensor_tensor(partial[:, 256:512], first[:, 256:512], second[:], ALU.add)
        first_quarter = gate_rest[:, 1, 0:P]
        nc.vector.tensor_tensor(first_quarter, picked(0, 0, P), gate_first[:, 0:P], ALU.mult)
        nc.vector.tensor_tensor(result[:, 256:512], partial[:, 256:512], third[:], ALU.add)
        store(256, 512)
        nc.vector.tensor_tensor(first[:, P:256], got_b[:], gate_first[:, P:256], ALU.mult)
        nc.vector.tensor_tensor(result[:, 0:128], first_quarter, back[0][:], ALU.add)
        nc.vector.tensor_tensor(result[:, 128:256], first[:, 128:256], back[1][:], ALU.add)
        store(0, 256)
